import numpy as np
import ml_dtypes


def mxq(x, axis, fmt="e4m3"):
    dtype, down = {"e4m3": (ml_dtypes.float8_e4m3fn, 7), "e5m2": (ml_dtypes.float8_e5m2, 14)}[fmt]
    v = np.moveaxis(np.asarray(x, np.float32).astype(ml_dtypes.bfloat16).astype(np.float64), axis, -1)
    blocks = v.reshape(v.shape[:-1] + (-1, 32))
    amax = np.abs(blocks).max(-1, keepdims=True)
    byte = np.maximum(np.where(amax > 0, np.frexp(amax)[1] - 1 + 127, 0) - down, 1)
    scale = np.exp2(byte - 127.0)
    codes = (blocks / scale).astype(np.float32).astype(dtype).astype(np.float64)
    return np.moveaxis((codes * scale).reshape(v.shape), -1, axis)


WIDE = False


def mx_kscale(k):
    if not WIDE:
        return np.ones(k)
    levels = np.array([10, -10, 5, -5, 0])
    if k % 512:
        return np.exp2(np.random.permutation(np.resize(levels, k // 32))).repeat(32)
    a = np.empty((k // 512, 16))
    for p in range(k // 512):
        a[p, :8] = np.random.permutation(np.resize(levels, 8))
        for g in range(8):
            far = levels[np.abs(levels - a[p, g]) >= 10]
            a[p, g + 8] = far[np.random.randint(len(far))]
    return np.exp2(a.ravel()).repeat(32)


def f64(x):
    return np.asarray(x).astype(np.float64)


def striped(idx):
    return np.tile(idx.reshape(-1, 16).T, (8, 1)).astype(np.uint16)


def unstriped(offs):
    return offs[:16].T.reshape(-1).astype(np.int64)


def striped8(idx):
    return np.concatenate([x.reshape(-1, 16).T for x in idx]).astype(np.uint16)


def runs(offs, k):
    lists = np.stack([offs[16 * r : 16 * r + 16].T.reshape(-1) for r in range(8)]).astype(np.int64)
    return lists[np.arange(k) % 512 // 64]


def pack_weight(w):
    k, n = w.shape
    w = f64(np.asarray(w, np.float32).astype(ml_dtypes.bfloat16)).reshape(k // 32, 32, n)
    amax = np.abs(w).max(1)
    byte = np.clip(np.where(amax > 0, np.frexp(amax)[1] - 1 + 127 - 7, 1), 1, 254)
    scaled = (w * np.exp2(127.0 - byte)[:, None, :]).reshape(k, n).astype(np.float32)
    words = np.ascontiguousarray(scaled.reshape(k // 512, 128, 4, n).transpose(0, 1, 3, 2)).astype(ml_dtypes.float8_e4m3fn).view(np.uint8)
    return words, np.ascontiguousarray(byte.astype(np.uint8).reshape(k // 512, 16, n))


def unpack_weight(words, scales):
    g, p, n, _ = words.shape
    vals = np.ascontiguousarray(words).view(ml_dtypes.float8_e4m3fn).astype(np.float64) * np.repeat(np.exp2(scales.astype(np.float64) - 127.0), 8, axis=1)[..., None]
    return vals.transpose(0, 1, 3, 2).reshape(g * 512, n)


def sigmoid(v):
    return 1.0 / (1.0 + np.exp(-np.maximum(v, -700.0)))


K, T, S, V, N, H = 512, 2048, 512, 512, 512, 512


def setup_inputs():
    n = np.random.standard_normal
    s = mx_kscale(K)[:, None]
    u = mx_kscale(S)
    packed_xT = pack_weight(n((K, T)) * s)
    return {
        "x_words": packed_xT[0],
        "x_scales": packed_xT[1],
        "w1": (n((K, H)) / np.sqrt(K) / s).astype(np.float32),
        "w2": (n((K, H)) / np.sqrt(K) / s).astype(np.float32),
        "gk": (np.random.uniform(0.5, 1.5, (H, 1)) * u[:, None]).astype(np.float32),
        "gq": (np.random.uniform(0.5, 1.5, (H, 1)) / u[:, None]).astype(np.float32),
        "wv": (n((K, N)) / np.sqrt(K) / s).astype(np.float32),
        "gi": (np.random.uniform(0.5, 1.5, (S, 1)) / u[:, None]).astype(np.float32),
        "res": n((N, V)).astype(np.float32),
        "gt": (np.random.uniform(0.5, 1.5, (S, 1)) * u[:, None]).astype(np.float32),
        "offs": striped(np.random.permutation(T)[:S]),
        "qs": striped(np.random.permutation(T)[:V]),
        "nb": striped8(np.stack([np.random.permutation(V) for _ in range(8)])),
    }


def reference(x_words, x_scales, w1, w2, gk, gq, wv, gi, res, gt, offs, qs, nb):
    xq = unpack_weight(x_words, x_scales)[:, unstriped(offs)]
    val = xq.T @ mxq(f64(wv), 0, "e4m3")
    zv = f64(gi) * val
    kf = mxq(f64(w1), 0, "e4m3").T @ xq
    z = f64(gk) * kf
    x_qs = unpack_weight(x_words, x_scales)[:, unstriped(qs)]
    qf = mxq(f64(w2), 0, "e4m3").T @ x_qs
    z2 = f64(gq) * qf
    s = 0.0625 * ((mxq(z, 0, "e4m3").T @ mxq(z2, 0, "e4m3")))
    zp = f64(gt) * (sigmoid(s + s[np.arange(S)[:, None], runs(nb, S)]))
    return f64(res) + 0.0625 * ((mxq(zv, 0, "e4m3").T @ mxq(zp, 0, "e4m3")))

@@ -1,0 +1,222 @@
+from contextlib import ExitStack
+
+import concourse.mybir as mybir
+from concourse.masks import make_identity
+
+K, T, S, V, N, H = 512, 2048, 512, 512, 512, 512
+FLOPS = 2 * K * S * N + 2 * K * H * S + 2 * K * H * V + 2 * H * S * V + 2 * S * N * V
+
+F32 = mybir.dt.float32
+BF16 = mybir.dt.bfloat16
+I32 = mybir.dt.int32
+U32 = mybir.dt.uint32
+U16 = mybir.dt.uint16
+U8 = mybir.dt.uint8
+FP8X4 = mybir.dt.float8_e4m3fn_x4
+ACT = mybir.ActivationFunctionType
+ALU = mybir.AluOpType
+
+P = 128
+PACK = 4
+RUN = 8
+CHUNK = 128
+GATHERS = ((0, 256), (256, 384), (384, 512))
+
+
+def tile_picked_listsmooth_sigmoid_p_kernel(
+    tc, x_words, x_scales, w1, w2, gk, gq, wv, gi, res, gt, offs, qs, nb, out
+):
+    nc = tc.nc
+    with ExitStack() as ctx:
+        keep = ctx.enter_context(tc.tile_pool(name="keep", bufs=1))
+        psum = ctx.enter_context(tc.psum_pool(name="psum", bufs=1))
+
+        def sb(name, shape, dtype):
+            return keep.tile(shape, dtype, name=name, align_bytes=64)
+
+        def bank(number, shape):
+            return psum.tile(shape, F32, name=f"bank{number}", tag=f"bank{number}")
+
+        offs_sb = sb("offs_sb", [P, S // 16], U16)
+        qs_sb = sb("qs_sb", [P, V // 16], U16)
+        nb_sb = sb("nb_sb", [P, V // 16], U16)
+        x_sc = sb("x_sc", [P, T], U8)
+        x_wd = keep.tile([P, T], I32, name="x_wd", tag="stage_x", align_bytes=64)
+        warm = keep.tile([P, 1], F32, name="warm", tag="stage_c", align_bytes=64)
+        raw = {}
+        gain_rows = sb("gain_rows", [P, P], F32)
+        ident = sb("ident", [P, P], F32)
+        gains = sb("gains", [P, 4 * PACK], F32)
+        zero = sb("zero", [P, 1], F32)
+
+        nc.gpsimd.memset(gain_rows[:], 0.0)
+        nc.gpsimd.memset(x_sc[:].bitcast(I32), 0)
+        make_identity(nc, ident[:])
+        nc.vector.memset(zero[:], 0.0)
+        nc.scalar.activation(warm[:], zero[:], ACT.Sigmoid)
+
+        def load_weights(name, w, tags):
+            width = 512 // len(tags)
+            for part, tag in enumerate(tags):
+                raw[name, part] = keep.tile([P, PACK, width], F32, name=f"{name}_raw{part}", tag=tag, align_bytes=64)
+                nc.sync.dma_start(raw[name, part][:], w.rearrange("(p j) c -> p j c", j=PACK)[:, :, width * part : width * (part + 1)])
+
+        nc.sync.dma_start(offs_sb[:], offs)
+        nc.sync.dma_start(qs_sb[:], qs)
+        nc.sync.dma_start(nb_sb[:], nb)
+        nc.sync.dma_start(x_wd[:], x_words[0].rearrange("p c r -> p (c r)").bitcast(I32))
+        for number, vec in enumerate((gk, gq, gi, gt)):
+            nc.sync.dma_start(
+                gain_rows[PACK * number : PACK * (number + 1), :].rearrange("t (b r) -> t b r", r=RUN),
+                vec.rearrange("(b t r) o -> t b (r o)", t=PACK, r=RUN),
+            )
+        load_weights("w1", w1, ("stage_a", "stage_b"))
+        for q in range(4):
+            nc.sync.dma_start(x_sc[32 * q : 32 * q + 4, :].bitcast(I32), x_scales[0, 4 * q : 4 * q + 4, :].bitcast(I32))
+        load_weights("w2", w2, ("stage_c",))
+
+        turned = bank(7, [P, P])
+        nc.tensor.transpose(turned[:], gain_rows[:], ident[:])
+        nc.scalar.copy(gains[:], turned[:, 0 : 4 * PACK])
+
+        def gain(number, columns):
+            return gains[:, PACK * number : PACK * (number + 1)].unsqueeze(1).to_broadcast([P, columns, PACK])
+
+        key_sc_listed = sb("key_sc_listed", [P, S], U8)
+        key_sc = sb("key_sc", [P, S], U8)
+        key_wd = sb("key_wd", [P, S], U32)
+        query_sc = sb("query_sc", [P, V], U8)
+        query_wd = sb("query_wd", [P, V], U32)
+        nc.vector.tensor_copy(
+            key_wd[:].rearrange("p (t b r) -> p b t r", t=PACK, r=RUN),
+            x_wd[:].bitcast(U32).indirect(offs_sb[:]),
+        )
+        nc.vector.tensor_copy(query_wd[:], x_wd[:].bitcast(U32).indirect(qs_sb[:]))
+        nc.vector.tensor_copy(key_sc_listed[:], x_sc[:].indirect(offs_sb[:]))
+        nc.vector.tensor_copy(
+            key_sc[:].bitcast(I32).rearrange("p (t b r) -> p t b r", t=PACK, r=RUN // 4),
+            key_sc_listed[:].bitcast(I32).rearrange("p (b t r) -> p t b r", t=PACK, r=RUN // 4),
+        )
+
+        def mx_pair(name):
+            return sb(name + "_wd", [P, 512], U32), sb(name + "_sc", [P, 512], U8)
+
+        def quantize(pair, grouped, cols):
+            nc.vector.quantize_mx(
+                out=pair[0][:, cols].bitcast(FP8X4),
+                scales=pair[1][:, cols],
+                in_=grouped[:, cols, :].rearrange("p c j -> p (c j)"),
+            )
+
+        def product(acc, left, left_cols, right, right_cols):
+            nc.tensor.matmul_mx(
+                out=acc,
+                lhsT=left[0][:, left_cols].bitcast(FP8X4),
+                lhsT_scale=left[1][:, left_cols],
+                rhs=right[0][:, right_cols].bitcast(FP8X4),
+                rhs_scale=right[1][:, right_cols],
+                start=True,
+                stop=True,
+            )
+
+        def chunk(c):
+            return slice(c * CHUNK, (c + 1) * CHUNK)
+
+        def round_dealt(name, parts):
+            grouped = sb(name + "_bf", [P, 512, PACK], BF16)
+            blocks = 16 // parts
+            for part in range(parts):
+                nc.scalar.copy(
+                    grouped[:].rearrange("p (t b r) j -> p t b j r", t=PACK, r=RUN)[:, :, blocks * part : blocks * (part + 1)],
+                    raw[name, part][:].rearrange("p j (b t r) -> p t b j r", t=PACK, r=RUN),
+                )
+            return grouped
+
+        def weighted_product(name, left, right, number, first_bank):
+            grouped = sb(name + "_bf", [P, 512, PACK], BF16)
+            pair = mx_pair(name)
+            for c in range(4):
+                acc = bank(first_bank + c, [P, PACK, CHUNK])
+                for t in range(PACK):
+                    product(acc[:, t, :], left, chunk(t), right, chunk(c))
+                nc.vector.tensor_tensor(
+                    grouped[:, chunk(c), :], acc[:].rearrange("p t c -> p c t"), gain(number, CHUNK), ALU.mult
+                )
+            for half in range(2):
+                quantize(pair, grouped, slice(256 * half, 256 * (half + 1)))
+            return pair
+
+        keys = (key_wd, key_sc)
+        queries = (query_wd, query_sc)
+
+        w1_bf = round_dealt("w1", 2)
+        w1_q = mx_pair("w1_q")
+        quantize(w1_q, w1_bf, slice(0, H))
+        nc.vector.tensor_copy(query_sc[:], x_sc[:].indirect(qs_sb[:]))
+        w2_bf = round_dealt("w2", 1)
+        load_weights("wv", wv, ("stage_x",))
+        z_q = weighted_product("z", w1_q, keys, 0, 0)
+        w2_q = mx_pair("w2_q")
+        quantize(w2_q, w2_bf, slice(0, H))
+
+        wv_bf = sb("wv_bf", [P, N, PACK], BF16)
+        nc.scalar.copy(
+            wv_bf[:].rearrange("p (c r) j -> p c j r", r=RUN),
+            raw["wv", 0][:].rearrange("p j (c r) -> p c j r", r=RUN),
+        )
+        res_sb = keep.tile([P, PACK, V], F32, name="res_sb", tag="stage_a", align_bytes=64)
+        nc.sync.dma_start(res_sb[:], res.rearrange("(m p) v -> p m v", p=P))
+        z2_q = weighted_product("z2", w2_q, queries, 1, 4)
+
+        wv_q = mx_pair("wv_q")
+        quantize(wv_q, wv_bf, slice(0, N))
+        zv_planes = sb("zv_planes", [P, PACK, N], BF16)
+        for t in range(PACK):
+            acc = bank(t, [P, N])
+            product(acc[:], keys, chunk(t), wv_q, slice(0, N))
+            nc.scalar.activation(zv_planes[:, t, :], acc[:], ACT.Copy, scale=gains[:, 2 * PACK + t : 2 * PACK + t + 1])
+
+        windows, plains = [], []
+        for t in range(PACK):
+            acc = bank(4 + t, [P, V])
+            product(acc[:], z_q, chunk(t), z2_q, slice(0, V))
+            window = sb(f"window{t}", [P, V], F32)
+            plain = sb(f"plain{t}", [P, V], F32)
+            nc.scalar.copy(window[:], acc[:])
+            nc.scalar.copy(plain[:], acc[:])
+            windows.append(window)
+            plains.append(plain)
+
+        zv_bf = sb("zv_bf", [P, N, PACK], BF16)
+        zv_q = mx_pair("zv")
+        nc.vector.tensor_copy(
+            zv_bf[:].rearrange("p (c i) t -> p c t i", i=4), zv_planes[:].rearrange("p t (c i) -> p c t i", i=4)
+        )
+        quantize(zv_q, zv_bf, slice(0, N))
+
+        joined = sb("joined", [P, PACK, V], F32)
+        gated = sb("gated", [P, V, PACK], F32)
+        zp_bf = sb("zp_bf", [P, V, PACK], BF16)
+        zp_q = mx_pair("zp")
+        for lo, hi in GATHERS:
+            for t in range(PACK):
+                nc.vector.tensor_tensor(
+                    joined[:, t, lo:hi], windows[t][:].indirect(nb_sb[:, lo // 16 : hi // 16]), plains[t][:, lo:hi], ALU.add
+                )
+            nc.scalar.activation(
+                gated[:, lo:hi, :].rearrange("p (c i) t -> p c t i", i=4),
+                joined[:, :, lo:hi].rearrange("p t (c i) -> p c t i", i=4),
+                ACT.Sigmoid,
+                scale=0.0625,
+            )
+        out_view = out.rearrange("(m p) v -> p m v", p=P)
+        for lo, hi in GATHERS:
+            nc.vector.tensor_tensor(zp_bf[:, lo:hi, :], gated[:, lo:hi, :], gain(3, hi - lo), ALU.mult)
+            quantize(zp_q, zp_bf, slice(lo, hi))
+            for c in range(lo // CHUNK, hi // CHUNK):
+                acc = bank(c, [P, PACK, CHUNK])
+                for m in range(PACK):
+                    product(acc[:, m, :], zv_q, chunk(m), zp_q, chunk(c))
+                result = sb(f"result{c}", [P, PACK, CHUNK], F32)
+                nc.vector.scalar_tensor_tensor(result[:], acc[:], 0.0625, res_sb[:, :, chunk(c)], ALU.mult, ALU.add)
+                nc.sync.dma_start(out_view[:, :, chunk(c)], result[:])

@@ -1,7 +1,6 @@
 from contextlib import ExitStack
 
 import concourse.mybir as mybir
-from concourse.masks import make_identity
 
 K, T, S, V, N, H = 512, 2048, 512, 512, 512, 512
 FLOPS = 2 * K * S * N + 2 * K * H * S + 2 * K * H * V + 2 * H * S * V + 2 * S * N * V
@@ -18,7 +17,7 @@ ALU = mybir.AluOpType
 
 P = 128
 PACK = 4
-RUN = 8
+RUN = 4
 CHUNK = 128
 GATHERS = ((0, 256), (256, 384), (384, 512))
 
@@ -31,8 +30,8 @@ def tile_picked_listsmooth_sigmoid_p_kernel(
         keep = ctx.enter_context(tc.tile_pool(name="keep", bufs=1))
         psum = ctx.enter_context(tc.psum_pool(name="psum", bufs=1))
 
-        def sb(name, shape, dtype):
-            return keep.tile(shape, dtype, name=name, align_bytes=64)
+        def sb(name, shape, dtype, tag=None):
+            return keep.tile(shape, dtype, name=name, tag=tag or name, align_bytes=64)
 
         def bank(number, shape):
             return psum.tile(shape, F32, name=f"bank{number}", tag=f"bank{number}")
@@ -41,43 +40,48 @@ def tile_picked_listsmooth_sigmoid_p_kernel(
         qs_sb = sb("qs_sb", [P, V // 16], U16)
         nb_sb = sb("nb_sb", [P, V // 16], U16)
         x_sc = sb("x_sc", [P, T], U8)
-        x_wd = keep.tile([P, T], I32, name="x_wd", tag="stage_x", align_bytes=64)
-        warm = keep.tile([P, 1], F32, name="warm", tag="stage_c", align_bytes=64)
+        x_wd = sb("x_wd", [P, T], I32)
         raw = {}
-        gain_rows = sb("gain_rows", [P, P], F32)
+        gain_rows = sb("gain_rows", [4, 512], F32, "stage_g")
+        gain_dealt = sb("gain_dealt", [P, 512], F32, "stage_x")
         ident = sb("ident", [P, P], F32)
         gains = sb("gains", [P, 4 * PACK], F32)
-        zero = sb("zero", [P, 1], F32)
+        zeros = sb("zeros", [P, P], F32, "stage_a")
 
-        nc.gpsimd.memset(gain_rows[:], 0.0)
-        nc.gpsimd.memset(x_sc[:].bitcast(I32), 0)
-        make_identity(nc, ident[:])
-        nc.vector.memset(zero[:], 0.0)
-        nc.scalar.activation(warm[:], zero[:], ACT.Sigmoid)
+        nc.vector.memset(x_sc[:].bitcast(I32), 0)
+        nc.gpsimd.memset(zeros[:], 0.0)
+        warm = sb("warm", [P, 1], F32)
+        nc.scalar.activation(warm[:], zeros[:, 0:1], ACT.Sigmoid)
+        nc.gpsimd.memset(gain_dealt[:], 0.0)
+        nc.gpsimd.affine_select(
+            out=ident[:], in_=zeros[:], compare_op=ALU.not_equal, fill=1.0, base=0, pattern=[[-1, P]], channel_multiplier=1
+        )
 
-        def load_weights(name, w, tags):
-            width = 512 // len(tags)
-            for part, tag in enumerate(tags):
-                raw[name, part] = keep.tile([P, PACK, width], F32, name=f"{name}_raw{part}", tag=tag, align_bytes=64)
-                nc.sync.dma_start(raw[name, part][:], w.rearrange("(p j) c -> p j c", j=PACK)[:, :, width * part : width * (part + 1)])
+        def load_weights(name, w, parts, tag):
+            width = 512 // parts
+            raw[name] = sb(name + "_raw", [P, parts, PACK, width], F32, tag)
+            for part in range(parts):
+                nc.sync.dma_start(raw[name][:, part], w.rearrange("(p j) c -> p j c", j=PACK)[:, :, width * part : width * (part + 1)])
 
         nc.sync.dma_start(offs_sb[:], offs)
         nc.sync.dma_start(qs_sb[:], qs)
-        nc.sync.dma_start(nb_sb[:], nb)
-        nc.sync.dma_start(x_wd[:], x_words[0].rearrange("p c r -> p (c r)").bitcast(I32))
         for number, vec in enumerate((gk, gq, gi, gt)):
-            nc.sync.dma_start(
-                gain_rows[PACK * number : PACK * (number + 1), :].rearrange("t (b r) -> t b r", r=RUN),
-                vec.rearrange("(b t r) o -> t b (r o)", t=PACK, r=RUN),
-            )
-        load_weights("w1", w1, ("stage_a", "stage_b"))
+            nc.sync.dma_start(gain_rows[number : number + 1, :], vec.rearrange("c o -> o c"))
+        nc.sync.dma_start(x_wd[:], x_words[0].rearrange("p c r -> p (c r)").bitcast(I32))
         for q in range(4):
             nc.sync.dma_start(x_sc[32 * q : 32 * q + 4, :].bitcast(I32), x_scales[0, 4 * q : 4 * q + 4, :].bitcast(I32))
-        load_weights("w2", w2, ("stage_c",))
+        load_weights("w1", w1, 2, "stage_a")
+        nc.sync.dma_start(nb_sb[:], nb)
 
-        turned = bank(7, [P, P])
-        nc.tensor.transpose(turned[:], gain_rows[:], ident[:])
-        nc.scalar.copy(gains[:], turned[:, 0 : 4 * PACK])
+        nc.scalar.copy(
+            gain_dealt[0:4, :].rearrange("n (t b r) -> n t b r", t=PACK, r=RUN),
+            gain_rows[:].rearrange("n (b t r) -> n t b r", t=PACK, r=RUN),
+        )
+        load_weights("w2", w2, 2, "stage_g")
+        turned = bank(7, [P, PACK, P])
+        for t in range(PACK):
+            nc.tensor.transpose(turned[:, t, :], gain_dealt[:, t * P : (t + 1) * P], ident[:])
+        nc.scalar.copy(gains[:].rearrange("p (n t) -> p n t", t=PACK), turned[:, :, 0:4].rearrange("p t n -> p n t"))
 
         def gain(number, columns):
             return gains[:, PACK * number : PACK * (number + 1)].unsqueeze(1).to_broadcast([P, columns, PACK])
@@ -85,18 +89,19 @@ def tile_picked_listsmooth_sigmoid_p_kernel(
         key_sc_listed = sb("key_sc_listed", [P, S], U8)
         key_sc = sb("key_sc", [P, S], U8)
         key_wd = sb("key_wd", [P, S], U32)
-        query_sc = sb("query_sc", [P, V], U8)
         query_wd = sb("query_wd", [P, V], U32)
         nc.vector.tensor_copy(
             key_wd[:].rearrange("p (t b r) -> p b t r", t=PACK, r=RUN),
             x_wd[:].bitcast(U32).indirect(offs_sb[:]),
         )
-        nc.vector.tensor_copy(query_wd[:], x_wd[:].bitcast(U32).indirect(qs_sb[:]))
         nc.vector.tensor_copy(key_sc_listed[:], x_sc[:].indirect(offs_sb[:]))
+        nc.vector.tensor_copy(query_wd[:], x_wd[:].bitcast(U32).indirect(qs_sb[:]))
         nc.vector.tensor_copy(
             key_sc[:].bitcast(I32).rearrange("p (t b r) -> p t b r", t=PACK, r=RUN // 4),
             key_sc_listed[:].bitcast(I32).rearrange("p (b t r) -> p t b r", t=PACK, r=RUN // 4),
         )
+
+        load_weights("wv", wv, 2, "stage_x")
 
         def mx_pair(name):
             return sb(name + "_wd", [P, 512], U32), sb(name + "_sc", [P, 512], U8)
@@ -124,68 +129,76 @@ def tile_picked_listsmooth_sigmoid_p_kernel(
 
         def round_dealt(name, parts):
             grouped = sb(name + "_bf", [P, 512, PACK], BF16)
-            blocks = 16 // parts
+            blocks = P // RUN // parts
             for part in range(parts):
                 nc.scalar.copy(
                     grouped[:].rearrange("p (t b r) j -> p t b j r", t=PACK, r=RUN)[:, :, blocks * part : blocks * (part + 1)],
-                    raw[name, part][:].rearrange("p j (b t r) -> p t b j r", t=PACK, r=RUN),
+                    raw[name][:, part].rearrange("p j (b t r) -> p t b j r", t=PACK, r=RUN),
                 )
             return grouped
 
-        def weighted_product(name, left, right, number, first_bank):
-            grouped = sb(name + "_bf", [P, 512, PACK], BF16)
-            pair = mx_pair(name)
-            for c in range(4):
-                acc = bank(first_bank + c, [P, PACK, CHUNK])
-                for t in range(PACK):
-                    product(acc[:, t, :], left, chunk(t), right, chunk(c))
-                nc.vector.tensor_tensor(
-                    grouped[:, chunk(c), :], acc[:].rearrange("p t c -> p c t"), gain(number, CHUNK), ALU.mult
-                )
-            for half in range(2):
-                quantize(pair, grouped, slice(256 * half, 256 * (half + 1)))
-            return pair
+        def weighted_chunk(grouped, left, right, number, c, bank_number):
+            acc = bank(bank_number, [P, PACK, CHUNK])
+            for t in range(PACK):
+                product(acc[:, t, :], left, chunk(t), right, chunk(c))
+            nc.vector.tensor_tensor(
+                grouped[:, chunk(c), :], acc[:].rearrange("p t c -> p c t"), gain(number, CHUNK), ALU.mult
+            )
 
         keys = (key_wd, key_sc)
-        queries = (query_wd, query_sc)
 
         w1_bf = round_dealt("w1", 2)
+        res_sb = sb("res_sb", [P, PACK, V], F32, "stage_a")
+        nc.sync.dma_start(res_sb[:], res.rearrange("(m p) v -> p m v", p=P))
         w1_q = mx_pair("w1_q")
         quantize(w1_q, w1_bf, slice(0, H))
+        query_sc = sb("query_sc", [P, V], U8, "w1_bf")
         nc.vector.tensor_copy(query_sc[:], x_sc[:].indirect(qs_sb[:]))
-        w2_bf = round_dealt("w2", 1)
-        load_weights("wv", wv, ("stage_x",))
-        z_q = weighted_product("z", w1_q, keys, 0, 0)
+        queries = (query_wd, query_sc)
+        w2_bf = round_dealt("w2", 2)
         w2_q = mx_pair("w2_q")
         quantize(w2_q, w2_bf, slice(0, H))
+        z_bf = sb("z_bf", [P, S, PACK], BF16)
+        for c in range(4):
+            weighted_chunk(z_bf, w1_q, keys, 0, c, c)
 
-        wv_bf = sb("wv_bf", [P, N, PACK], BF16)
-        nc.scalar.copy(
-            wv_bf[:].rearrange("p (c r) j -> p c j r", r=RUN),
-            raw["wv", 0][:].rearrange("p j (c r) -> p c j r", r=RUN),
-        )
-        res_sb = keep.tile([P, PACK, V], F32, name="res_sb", tag="stage_a", align_bytes=64)
-        nc.sync.dma_start(res_sb[:], res.rearrange("(m p) v -> p m v", p=P))
-        z2_q = weighted_product("z2", w2_q, queries, 1, 4)
+        wv_bf = sb("wv_bf", [P, N, PACK], BF16, "grouped")
+        for part in range(2):
+            nc.scalar.copy(
+                wv_bf[:, 256 * part : 256 * (part + 1), :].rearrange("p (c r) j -> p c j r", r=RUN),
+                raw["wv"][:, part].rearrange("p j (c r) -> p c j r", r=RUN),
+            )
 
         wv_q = mx_pair("wv_q")
         quantize(wv_q, wv_bf, slice(0, N))
+        z_q = (sb("z_wd", [P, S], U32, "grouped"), sb("z_sc", [P, S], U8))
+        quantize(z_q, z_bf, slice(0, S))
+
+        z2_bf = sb("z2_bf", [P, V, PACK], BF16)
+        z2_q = mx_pair("z2")
+        windows = [sb(f"window{t}", [P, V], F32) for t in range(PACK)]
+        plains = [[sb(f"plain{t}_{half}", [P, 256], F32) for half in range(2)] for t in range(PACK)]
+        for c in range(4):
+            weighted_chunk(z2_bf, w2_q, queries, 1, c, 4 + c)
+            if c % 2 == 0:
+                continue
+            half = c // 2
+            cols = slice(256 * half, 256 * (half + 1))
+            quantize(z2_q, z2_bf, cols)
+            for pair in range(2):
+                acc = bank(4 + 2 * half + pair, [P, 2, 256])
+                for u in range(2):
+                    product(acc[:, u, :], z_q, chunk(2 * pair + u), z2_q, cols)
+                for u in range(2):
+                    t = 2 * pair + u
+                    nc.scalar.copy(windows[t][:, cols], acc[:, u, :])
+                    nc.sync.dma_start(plains[t][half][:], windows[t][:, cols])
+
         zv_planes = sb("zv_planes", [P, PACK, N], BF16)
         for t in range(PACK):
             acc = bank(t, [P, N])
             product(acc[:], keys, chunk(t), wv_q, slice(0, N))
             nc.scalar.activation(zv_planes[:, t, :], acc[:], ACT.Copy, scale=gains[:, 2 * PACK + t : 2 * PACK + t + 1])
-
-        windows, plains = [], []
-        for t in range(PACK):
-            acc = bank(4 + t, [P, V])
-            product(acc[:], z_q, chunk(t), z2_q, slice(0, V))
-            window = sb(f"window{t}", [P, V], F32)
-            plain = sb(f"plain{t}", [P, V], F32)
-            nc.scalar.copy(window[:], acc[:])
-            nc.scalar.copy(plain[:], acc[:])
-            windows.append(window)
-            plains.append(plain)
 
         zv_bf = sb("zv_bf", [P, N, PACK], BF16)
         zv_q = mx_pair("zv")
@@ -195,28 +208,39 @@ def tile_picked_listsmooth_sigmoid_p_kernel(
         quantize(zv_q, zv_bf, slice(0, N))
 
         joined = sb("joined", [P, PACK, V], F32)
-        gated = sb("gated", [P, V, PACK], F32)
-        zp_bf = sb("zp_bf", [P, V, PACK], BF16)
+        gated = sb("gated", [P, PACK, V], F32)
+        zp_planes, zp_bf = {}, {}
         zp_q = mx_pair("zp")
         for lo, hi in GATHERS:
             for t in range(PACK):
                 nc.vector.tensor_tensor(
-                    joined[:, t, lo:hi], windows[t][:].indirect(nb_sb[:, lo // 16 : hi // 16]), plains[t][:, lo:hi], ALU.add
+                    joined[:, t, lo:hi], windows[t][:].indirect(nb_sb[:, lo // 16 : hi // 16]), plains[t][lo // 256][:, lo % 256 : lo % 256 + hi - lo], ALU.add
                 )
-            nc.scalar.activation(
-                gated[:, lo:hi, :].rearrange("p (c i) t -> p c t i", i=4),
-                joined[:, :, lo:hi].rearrange("p t (c i) -> p c t i", i=4),
-                ACT.Sigmoid,
-                scale=0.0625,
-            )
+            nc.scalar.activation(gated[:, :, lo:hi], joined[:, :, lo:hi], ACT.Sigmoid, scale=0.0625)
+            zp_planes[lo] = sb(f"zp_planes{lo}", [P, PACK, hi - lo], BF16)
+            for t in range(PACK):
+                nc.scalar.activation(zp_planes[lo][:, t, :], gated[:, t, lo:hi], ACT.Copy, scale=gains[:, 3 * PACK + t : 3 * PACK + t + 1])
         out_view = out.rearrange("(m p) v -> p m v", p=P)
         for lo, hi in GATHERS:
-            nc.vector.tensor_tensor(zp_bf[:, lo:hi, :], gated[:, lo:hi, :], gain(3, hi - lo), ALU.mult)
-            quantize(zp_q, zp_bf, slice(lo, hi))
-            for c in range(lo // CHUNK, hi // CHUNK):
-                acc = bank(c, [P, PACK, CHUNK])
-                for m in range(PACK):
-                    product(acc[:, m, :], zv_q, chunk(m), zp_q, chunk(c))
-                result = sb(f"result{c}", [P, PACK, CHUNK], F32)
-                nc.vector.scalar_tensor_tensor(result[:], acc[:], 0.0625, res_sb[:, :, chunk(c)], ALU.mult, ALU.add)
-                nc.sync.dma_start(out_view[:, :, chunk(c)], result[:])
+            zp_bf[lo] = sb(f"zp_bf{lo}", [P, hi - lo, PACK], BF16)
+            nc.vector.tensor_copy(
+                zp_bf[lo][:].rearrange("p (c i) t -> p c t i", i=4),
+                zp_planes[lo][:].rearrange("p t (c i) -> p c t i", i=4),
+            )
+            nc.vector.quantize_mx(
+                out=zp_q[0][:, lo:hi].bitcast(FP8X4),
+                scales=zp_q[1][:, lo:hi],
+                in_=zp_bf[lo][:].rearrange("p c j -> p (c j)"),
+            )
+        spent = ("zp_bf256", "zp_planes256", "zp_bf384", "result")
+        for lo, hi in GATHERS:
+            width = hi - lo
+            rows = 512 // width
+            for m0 in range(0, PACK, rows):
+                number = lo // CHUNK + m0 // rows
+                acc = bank(number, [P, rows, width])
+                for m in range(rows):
+                    product(acc[:, m, :], zv_q, chunk(m0 + m), zp_q, slice(lo, hi))
+                result = sb(f"result{number}", [P, rows, width], F32, spent[number])
+                nc.vector.scalar_tensor_tensor(result[:], acc[:], 0.0625, res_sb[:, m0 : m0 + rows, lo:hi], ALU.mult, ALU.add)
+                nc.sync.dma_start(out_view[:, m0 : m0 + rows, lo:hi], result[:])

@@ -17,9 +17,8 @@ ALU = mybir.AluOpType
 
 P = 128
 PACK = 4
-RUN = 4
-CHUNK = 128
-GATHERS = ((0, 256), (256, 384), (384, 512))
+HALF = 256
+RANGES = ((0, 256), (256, 384), (384, 512))
 
 
 def tile_picked_listsmooth_sigmoid_p_kernel(
@@ -36,81 +35,59 @@ def tile_picked_listsmooth_sigmoid_p_kernel(
         def bank(number, shape):
             return psum.tile(shape, F32, name=f"bank{number}", tag=f"bank{number}")
 
-        offs_sb = sb("offs_sb", [P, S // 16], U16)
-        qs_sb = sb("qs_sb", [P, V // 16], U16)
-        nb_sb = sb("nb_sb", [P, V // 16], U16)
+        def chunk(c):
+            return slice(c * P, (c + 1) * P)
+
+        def load_list(name, src):
+            tile = sb(name, [P, 32], U16)
+            nc.sync.dma_start(tile[:], src)
+            return tile
+
+        def load_gain(name, src):
+            tile = sb(name, [P, PACK], F32)
+            nc.sync.dma_start(tile[:], src.rearrange("(p t) o -> p (t o)", t=PACK))
+            return tile
+
+        def load_halves(halves, w):
+            rows = w.rearrange("(p j) c -> p j c", j=PACK)
+            for part in range(2):
+                nc.sync.dma_start(halves[part][:], rows[:, :, HALF * part : HALF * (part + 1)])
+
+        sc_rows = sb("sc_rows", [P, T // 4], I32)
         x_sc = sb("x_sc", [P, T], U8)
         x_wd = sb("x_wd", [P, T], I32)
-        raw = {}
-        gain_rows = sb("gain_rows", [4, 512], F32, "stage_g")
-        gain_dealt = sb("gain_dealt", [P, 512], F32, "stage_x")
-        ident = sb("ident", [P, P], F32)
-        gains = sb("gains", [P, 4 * PACK], F32)
-        zeros = sb("zeros", [P, P], F32, "stage_a")
-
-        nc.vector.memset(x_sc[:].bitcast(I32), 0)
-        nc.gpsimd.memset(zeros[:], 0.0)
+        cold = sb("cold", [P, 1], F32)
         warm = sb("warm", [P, 1], F32)
-        nc.scalar.activation(warm[:], zeros[:, 0:1], ACT.Sigmoid)
-        nc.gpsimd.memset(gain_dealt[:], 0.0)
-        nc.gpsimd.affine_select(
-            out=ident[:], in_=zeros[:], compare_op=ALU.not_equal, fill=1.0, base=0, pattern=[[-1, P]], channel_multiplier=1
-        )
-
-        def load_weights(name, w, parts, tag):
-            width = 512 // parts
-            raw[name] = sb(name + "_raw", [P, parts, PACK, width], F32, tag)
-            for part in range(parts):
-                nc.sync.dma_start(raw[name][:, part], w.rearrange("(p j) c -> p j c", j=PACK)[:, :, width * part : width * (part + 1)])
-
-        nc.sync.dma_start(offs_sb[:], offs)
-        nc.sync.dma_start(qs_sb[:], qs)
-        for number, vec in enumerate((gk, gq, gi, gt)):
-            nc.sync.dma_start(gain_rows[number : number + 1, :], vec.rearrange("c o -> o c"))
-        nc.sync.dma_start(x_wd[:], x_words[0].rearrange("p c r -> p (c r)").bitcast(I32))
+        qs_sb = load_list("qs_sb", qs)
+        offs_sb = load_list("offs_sb", offs)
+        for q, queue in enumerate((nc.scalar, nc.scalar, nc.sync, nc.sync)):
+            queue.dma_start(sc_rows[32 * q : 32 * q + 4, :], x_scales[0, 4 * q : 4 * q + 4, :].bitcast(I32))
+        nc.gpsimd.memset(cold[:], 0.0)
+        nc.scalar.activation(warm[:], cold[:], ACT.Sigmoid)
+        nc.vector.memset(x_sc[:].bitcast(I32), 0)
         for q in range(4):
-            nc.sync.dma_start(x_sc[32 * q : 32 * q + 4, :].bitcast(I32), x_scales[0, 4 * q : 4 * q + 4, :].bitcast(I32))
-        load_weights("w1", w1, 2, "stage_a")
-        nc.sync.dma_start(nb_sb[:], nb)
-
-        nc.scalar.copy(
-            gain_dealt[0:4, :].rearrange("n (t b r) -> n t b r", t=PACK, r=RUN),
-            gain_rows[:].rearrange("n (b t r) -> n t b r", t=PACK, r=RUN),
-        )
-        load_weights("w2", w2, 2, "stage_g")
-        turned = bank(7, [P, PACK, P])
-        for t in range(PACK):
-            nc.tensor.transpose(turned[:, t, :], gain_dealt[:, t * P : (t + 1) * P], ident[:])
-        nc.scalar.copy(gains[:].rearrange("p (n t) -> p n t", t=PACK), turned[:, :, 0:4].rearrange("p t n -> p n t"))
-
-        def gain(number, columns):
-            return gains[:, PACK * number : PACK * (number + 1)].unsqueeze(1).to_broadcast([P, columns, PACK])
-
-        key_sc_listed = sb("key_sc_listed", [P, S], U8)
-        key_sc = sb("key_sc", [P, S], U8)
-        key_wd = sb("key_wd", [P, S], U32)
-        query_wd = sb("query_wd", [P, V], U32)
-        nc.vector.tensor_copy(
-            key_wd[:].rearrange("p (t b r) -> p b t r", t=PACK, r=RUN),
-            x_wd[:].bitcast(U32).indirect(offs_sb[:]),
-        )
-        nc.vector.tensor_copy(key_sc_listed[:], x_sc[:].indirect(offs_sb[:]))
-        nc.vector.tensor_copy(query_wd[:], x_wd[:].bitcast(U32).indirect(qs_sb[:]))
-        nc.vector.tensor_copy(
-            key_sc[:].bitcast(I32).rearrange("p (t b r) -> p t b r", t=PACK, r=RUN // 4),
-            key_sc_listed[:].bitcast(I32).rearrange("p (b t r) -> p t b r", t=PACK, r=RUN // 4),
-        )
-
-        load_weights("wv", wv, 2, "stage_x")
+            nc.vector.tensor_copy(x_sc[32 * q : 32 * q + 4, :].bitcast(I32), sc_rows[32 * q : 32 * q + 4, :])
+        nc.sync.dma_start(x_wd[:], x_words[0].rearrange("p c r -> p (c r)").bitcast(I32))
+        w2_raw = [sb(f"w2_raw{part}", [P, PACK, HALF], F32) for part in range(2)]
+        load_halves(w2_raw, w2)
+        w1_raw = [sb(f"w1_raw{part}", [P, PACK, HALF], F32) for part in range(2)]
+        load_halves(w1_raw, w1)
+        gq_sb = load_gain("gq_sb", gq)
+        gk_sb = load_gain("gk_sb", gk)
+        wv_raw = [sb(f"wv_raw{part}", [P, PACK, HALF], F32) for part in range(2)]
+        load_halves(wv_raw, wv)
+        nb_sb = load_list("nb_sb", nb)
+        gi_sb = load_gain("gi_sb", gi)
+        gt_sb = load_gain("gt_sb", gt)
+        res_sb = sb("res_sb", [P, PACK, V], F32)
+        nc.sync.dma_start(res_sb[:], res.rearrange("(m p) v -> p m v", p=P))
 
         def mx_pair(name):
             return sb(name + "_wd", [P, 512], U32), sb(name + "_sc", [P, 512], U8)
 
-        def quantize(pair, grouped, cols):
+        def quantize(pair, cols, grouped):
             nc.vector.quantize_mx(
-                out=pair[0][:, cols].bitcast(FP8X4),
-                scales=pair[1][:, cols],
-                in_=grouped[:, cols, :].rearrange("p c j -> p (c j)"),
+                out=pair[0][:, cols].bitcast(FP8X4), scales=pair[1][:, cols], in_=grouped.rearrange("p c j -> p (c j)")
             )
 
         def product(acc, left, left_cols, right, right_cols):
@@ -124,123 +101,137 @@ def tile_picked_listsmooth_sigmoid_p_kernel(
                 stop=True,
             )
 
-        def chunk(c):
-            return slice(c * CHUNK, (c + 1) * CHUNK)
-
-        def round_dealt(name, parts):
+        def round_dealt(name, halves):
             grouped = sb(name + "_bf", [P, 512, PACK], BF16)
-            blocks = P // RUN // parts
-            for part in range(parts):
+            for part in range(2):
                 nc.scalar.copy(
-                    grouped[:].rearrange("p (t b r) j -> p t b j r", t=PACK, r=RUN)[:, :, blocks * part : blocks * (part + 1)],
-                    raw[name][:, part].rearrange("p j (b t r) -> p t b j r", t=PACK, r=RUN),
+                    grouped[:].rearrange("p (t m) j -> p m j t", t=PACK)[:, 64 * part : 64 * (part + 1)],
+                    halves[part][:].rearrange("p j (m t) -> p m j t", t=PACK),
                 )
             return grouped
 
-        def weighted_chunk(grouped, left, right, number, c, bank_number):
-            acc = bank(bank_number, [P, PACK, CHUNK])
-            for t in range(PACK):
-                product(acc[:, t, :], left, chunk(t), right, chunk(c))
+        def weighted_read(grouped, acc, gain):
             nc.vector.tensor_tensor(
-                grouped[:, chunk(c), :], acc[:].rearrange("p t c -> p c t"), gain(number, CHUNK), ALU.mult
+                grouped, acc[:].rearrange("p t c -> p c t"), gain[:].unsqueeze(1).to_broadcast([P, P, PACK]), ALU.mult
             )
 
-        keys = (key_wd, key_sc)
+        def interleave(grouped, planes):
+            nc.vector.tensor_copy(
+                grouped.rearrange("p (c i) t -> p c t i", i=4), planes.rearrange("p t (c i) -> p c t i", i=4)
+            )
 
-        w1_bf = round_dealt("w1", 2)
-        res_sb = sb("res_sb", [P, PACK, V], F32, "stage_a")
-        nc.sync.dma_start(res_sb[:], res.rearrange("(m p) v -> p m v", p=P))
-        w1_q = mx_pair("w1_q")
-        quantize(w1_q, w1_bf, slice(0, H))
-        query_sc = sb("query_sc", [P, V], U8, "w1_bf")
-        nc.vector.tensor_copy(query_sc[:], x_sc[:].indirect(qs_sb[:]))
-        queries = (query_wd, query_sc)
-        w2_bf = round_dealt("w2", 2)
+        keys = mx_pair("key")
+        queries = mx_pair("query")
+        key_sc_listed = sb("key_sc_listed", [P, S], U8)
+        nc.vector.tensor_copy(queries[1][:], x_sc[:].indirect(qs_sb[:]))
+        nc.vector.tensor_copy(key_sc_listed[:], x_sc[:].indirect(offs_sb[:]))
+        nc.vector.tensor_copy(queries[0][:], x_wd[:].bitcast(U32).indirect(qs_sb[:]))
+        nc.vector.tensor_copy(
+            keys[1][:].rearrange("p (t m) -> p m t", t=PACK), key_sc_listed[:].rearrange("p (m t) -> p m t", t=PACK)
+        )
+        nc.vector.tensor_copy(keys[0][:].rearrange("p (t m) -> p m t", t=PACK), x_wd[:].bitcast(U32).indirect(offs_sb[:]))
+
+        w2_bf = round_dealt("w2", w2_raw)
         w2_q = mx_pair("w2_q")
-        quantize(w2_q, w2_bf, slice(0, H))
-        z_bf = sb("z_bf", [P, S, PACK], BF16)
-        for c in range(4):
-            weighted_chunk(z_bf, w1_q, keys, 0, c, c)
-
-        wv_bf = sb("wv_bf", [P, N, PACK], BF16, "grouped")
-        for part in range(2):
-            nc.scalar.copy(
-                wv_bf[:, 256 * part : 256 * (part + 1), :].rearrange("p (c r) j -> p c j r", r=RUN),
-                raw["wv"][:, part].rearrange("p j (c r) -> p c j r", r=RUN),
-            )
-
-        wv_q = mx_pair("wv_q")
-        quantize(wv_q, wv_bf, slice(0, N))
-        z_q = (sb("z_wd", [P, S], U32, "grouped"), sb("z_sc", [P, S], U8))
-        quantize(z_q, z_bf, slice(0, S))
+        quantize(w2_q, slice(0, H), w2_bf[:])
+        w1_bf = round_dealt("w1", w1_raw)
+        w1_q = mx_pair("w1_q")
+        quantize(w1_q, slice(0, H), w1_bf[:])
 
         z2_bf = sb("z2_bf", [P, V, PACK], BF16)
-        z2_q = mx_pair("z2")
-        windows = [sb(f"window{t}", [P, V], F32) for t in range(PACK)]
-        plains = [[sb(f"plain{t}_{half}", [P, 256], F32) for half in range(2)] for t in range(PACK)]
+        z2_q = mx_pair("z2_q")
         for c in range(4):
-            weighted_chunk(z2_bf, w2_q, queries, 1, c, 4 + c)
-            if c % 2 == 0:
-                continue
-            half = c // 2
-            cols = slice(256 * half, 256 * (half + 1))
-            quantize(z2_q, z2_bf, cols)
-            for pair in range(2):
-                acc = bank(4 + 2 * half + pair, [P, 2, 256])
-                for u in range(2):
-                    product(acc[:, u, :], z_q, chunk(2 * pair + u), z2_q, cols)
-                for u in range(2):
-                    t = 2 * pair + u
-                    nc.scalar.copy(windows[t][:, cols], acc[:, u, :])
-                    nc.sync.dma_start(plains[t][half][:], windows[t][:, cols])
+            acc = bank(c, [P, PACK, P])
+            for t in range(PACK):
+                product(acc[:, t, :], w2_q, chunk(t), queries, chunk(c))
+            weighted_read(z2_bf[:, chunk(c), :], acc, gq_sb)
 
+        wv_bf = sb("wv_bf", [P, N, PACK], BF16)
+        for part in range(2):
+            nc.scalar.copy(
+                wv_bf[:, HALF * part : HALF * (part + 1), :].rearrange("p (c r) j -> p c j r", r=4),
+                wv_raw[part][:].rearrange("p j (c r) -> p c j r", r=4),
+            )
+        z_planes = sb("z_planes", [P, PACK, HALF], BF16)
+        for pair in range(2):
+            acc = bank(4 + pair, [P, 2, HALF])
+            for e in range(2):
+                product(acc[:, e, :], w1_q, chunk(2 * pair + e), keys, slice(HALF, S))
+            for e in range(2):
+                t = 2 * pair + e
+                nc.scalar.activation(z_planes[:, t, :], acc[:, e, :], ACT.Copy, scale=gk_sb[:, t : t + 1])
+        z_q = mx_pair("z_q")
+        z_bf = [sb(f"z_bf{half}", [P, HALF, PACK], BF16) for half in range(2)]
+        for u in range(2):
+            acc = bank(6 + u, [P, PACK, P])
+            for t in range(PACK):
+                product(acc[:, t, :], w1_q, chunk(t), keys, chunk(u))
+            weighted_read(z_bf[0][:, chunk(u), :], acc, gk_sb)
+        quantize(z2_q, slice(0, V), z2_bf[:])
+
+        windows = [sb(f"window{u}", [P, V], F32) for u in range(PACK)]
+        plains = [sb(f"plain{u}", [P, V], F32) for u in range(PACK)]
+
+        def scores(half):
+            quantize(z_q, slice(HALF * half, HALF * (half + 1)), z_bf[half][:])
+            for u in range(2 * half, 2 * half + 2):
+                acc = bank(u, [P, V])
+                product(acc[:], z_q, chunk(u), z2_q, slice(0, V))
+                nc.scalar.copy(windows[u][:], acc[:])
+
+        scores(0)
+        wv_q = mx_pair("wv_q")
+        interleave(z_bf[1][:], z_planes[:])
+        quantize(wv_q, slice(0, N), wv_bf[:])
+        scores(1)
+        for u in range(2, PACK):
+            nc.sync.dma_start(plains[u][:], windows[u][:])
         zv_planes = sb("zv_planes", [P, PACK, N], BF16)
-        for t in range(PACK):
-            acc = bank(t, [P, N])
-            product(acc[:], keys, chunk(t), wv_q, slice(0, N))
-            nc.scalar.activation(zv_planes[:, t, :], acc[:], ACT.Copy, scale=gains[:, 2 * PACK + t : 2 * PACK + t + 1])
+        for u in range(PACK):
+            acc = bank(4 + u, [P, N])
+            product(acc[:], keys, chunk(u), wv_q, slice(0, N))
+            nc.scalar.activation(zv_planes[:, u, :], acc[:], ACT.Copy, scale=gi_sb[:, u : u + 1])
 
+        zp_planes = sb("zp_planes", [P, PACK, V], BF16)
+        zp_q = mx_pair("zp_q")
+
+        def gate(u, ranges):
+            joined = sb(f"joined{u}", [P, V], F32)
+            gated = sb(f"gated{u}", [P, V], F32)
+            for lo, hi in ranges:
+                for first in range(lo, hi, HALF):
+                    last = min(first + HALF, hi)
+                    nc.vector.tensor_tensor(
+                        joined[:, first:last],
+                        windows[u][:].indirect(nb_sb[:, first // 16 : last // 16]),
+                        plains[u][:, first:last],
+                        ALU.add,
+                    )
+                nc.scalar.activation(gated[:, lo:hi], joined[:, lo:hi], ACT.Sigmoid, scale=0.0625)
+                nc.scalar.activation(zp_planes[:, u, lo:hi], gated[:, lo:hi], ACT.Copy, scale=gt_sb[:, u : u + 1])
+
+        for u in range(2):
+            nc.vector.tensor_copy(plains[u][:], windows[u][:])
+            gate(u, ((0, V),))
+        gate(2, ((0, V),))
         zv_bf = sb("zv_bf", [P, N, PACK], BF16)
-        zv_q = mx_pair("zv")
-        nc.vector.tensor_copy(
-            zv_bf[:].rearrange("p (c i) t -> p c t i", i=4), zv_planes[:].rearrange("p t (c i) -> p c t i", i=4)
-        )
-        quantize(zv_q, zv_bf, slice(0, N))
-
-        joined = sb("joined", [P, PACK, V], F32)
-        gated = sb("gated", [P, PACK, V], F32)
-        zp_planes, zp_bf = {}, {}
-        zp_q = mx_pair("zp")
-        for lo, hi in GATHERS:
-            for t in range(PACK):
-                nc.vector.tensor_tensor(
-                    joined[:, t, lo:hi], windows[t][:].indirect(nb_sb[:, lo // 16 : hi // 16]), plains[t][lo // 256][:, lo % 256 : lo % 256 + hi - lo], ALU.add
-                )
-            nc.scalar.activation(gated[:, :, lo:hi], joined[:, :, lo:hi], ACT.Sigmoid, scale=0.0625)
-            zp_planes[lo] = sb(f"zp_planes{lo}", [P, PACK, hi - lo], BF16)
-            for t in range(PACK):
-                nc.scalar.activation(zp_planes[lo][:, t, :], gated[:, t, lo:hi], ACT.Copy, scale=gains[:, 3 * PACK + t : 3 * PACK + t + 1])
+        zv_q = mx_pair("zv_q")
+        interleave(zv_bf[:], zv_planes[:])
+        gate(3, RANGES)
+        quantize(zv_q, slice(0, N), zv_bf[:])
         out_view = out.rearrange("(m p) v -> p m v", p=P)
-        for lo, hi in GATHERS:
-            zp_bf[lo] = sb(f"zp_bf{lo}", [P, hi - lo, PACK], BF16)
-            nc.vector.tensor_copy(
-                zp_bf[lo][:].rearrange("p (c i) t -> p c t i", i=4),
-                zp_planes[lo][:].rearrange("p t (c i) -> p c t i", i=4),
-            )
-            nc.vector.quantize_mx(
-                out=zp_q[0][:, lo:hi].bitcast(FP8X4),
-                scales=zp_q[1][:, lo:hi],
-                in_=zp_bf[lo][:].rearrange("p c j -> p (c j)"),
-            )
-        spent = ("zp_bf256", "zp_planes256", "zp_bf384", "result")
-        for lo, hi in GATHERS:
+        for lo, hi in RANGES:
+            zp_bf = sb(f"zp_bf{lo}", [P, hi - lo, PACK], BF16)
+            interleave(zp_bf[:], zp_planes[:, :, lo:hi])
+            quantize(zp_q, slice(lo, hi), zp_bf[:])
+        for lo, hi in RANGES:
             width = hi - lo
             rows = 512 // width
             for m0 in range(0, PACK, rows):
-                number = lo // CHUNK + m0 // rows
+                number = lo // P + m0 // rows
                 acc = bank(number, [P, rows, width])
                 for m in range(rows):
                     product(acc[:, m, :], zv_q, chunk(m0 + m), zp_q, slice(lo, hi))
-                result = sb(f"result{number}", [P, rows, width], F32, spent[number])
+                result = sb(f"result{number}", [P, rows, width], F32)
                 nc.vector.scalar_tensor_tensor(result[:], acc[:], 0.0625, res_sb[:, m0 : m0 + rows, lo:hi], ALU.mult, ALU.add)
                 nc.sync.dma_start(out_view[:, m0 : m0 + rows, lo:hi], result[:])

@@ -67,9 +67,9 @@ def tile_picked_listsmooth_sigmoid_p_kernel(
         nc.vector.memset(x_sc[:].bitcast(I32), 0)
         for q in range(4):
             nc.vector.tensor_copy(x_sc[32 * q : 32 * q + 4, :].bitcast(I32), sc_rows[32 * q : 32 * q + 4, :])
-        nc.sync.dma_start(x_wd[:], x_words[0].rearrange("p c r -> p (c r)").bitcast(I32))
         w2_raw = [sb(f"w2_raw{part}", [P, PACK, HALF], F32) for part in range(2)]
         load_halves(w2_raw, w2)
+        nc.sync.dma_start(x_wd[:], x_words[0].rearrange("p c r -> p (c r)").bitcast(I32))
         w1_raw = [sb(f"w1_raw{part}", [P, PACK, HALF], F32) for part in range(2)]
         load_halves(w1_raw, w1)
         gq_sb = load_gain("gq_sb", gq)
@@ -115,25 +115,22 @@ def tile_picked_listsmooth_sigmoid_p_kernel(
                 grouped, acc[:].rearrange("p t c -> p c t"), gain[:].unsqueeze(1).to_broadcast([P, P, PACK]), ALU.mult
             )
 
-        def interleave(grouped, planes):
-            nc.vector.tensor_copy(
-                grouped.rearrange("p (c i) t -> p c t i", i=4), planes.rearrange("p t (c i) -> p c t i", i=4)
-            )
+        def interleave(grouped, planes, move=nc.vector.tensor_copy):
+            move(grouped.rearrange("p (c i) t -> p c t i", i=4), planes.rearrange("p t (c i) -> p c t i", i=4))
 
         keys = mx_pair("key")
         queries = mx_pair("query")
         key_sc_listed = sb("key_sc_listed", [P, S], U8)
         nc.vector.tensor_copy(queries[1][:], x_sc[:].indirect(qs_sb[:]))
         nc.vector.tensor_copy(key_sc_listed[:], x_sc[:].indirect(offs_sb[:]))
-        nc.vector.tensor_copy(queries[0][:], x_wd[:].bitcast(U32).indirect(qs_sb[:]))
         nc.vector.tensor_copy(
             keys[1][:].rearrange("p (t m) -> p m t", t=PACK), key_sc_listed[:].rearrange("p (m t) -> p m t", t=PACK)
         )
-        nc.vector.tensor_copy(keys[0][:].rearrange("p (t m) -> p m t", t=PACK), x_wd[:].bitcast(U32).indirect(offs_sb[:]))
-
         w2_bf = round_dealt("w2", w2_raw)
         w2_q = mx_pair("w2_q")
         quantize(w2_q, slice(0, H), w2_bf[:])
+        nc.vector.tensor_copy(queries[0][:], x_wd[:].bitcast(U32).indirect(qs_sb[:]))
+        nc.vector.tensor_copy(keys[0][:].rearrange("p (t m) -> p m t", t=PACK), x_wd[:].bitcast(U32).indirect(offs_sb[:]))
         w1_bf = round_dealt("w1", w1_raw)
         w1_q = mx_pair("w1_q")
         quantize(w1_q, slice(0, H), w1_bf[:])
@@ -147,11 +144,14 @@ def tile_picked_listsmooth_sigmoid_p_kernel(
             weighted_read(z2_bf[:, chunk(c), :], acc, gq_sb)
 
         wv_bf = sb("wv_bf", [P, N, PACK], BF16)
-        for part in range(2):
+
+        def round_values(part):
             nc.scalar.copy(
                 wv_bf[:, HALF * part : HALF * (part + 1), :].rearrange("p (c r) j -> p c j r", r=4),
                 wv_raw[part][:].rearrange("p j (c r) -> p c j r", r=4),
             )
+
+        round_values(0)
         z_planes = sb("z_planes", [P, PACK, HALF], BF16)
         for pair in range(2):
             acc = bank(4 + pair, [P, 2, HALF])
@@ -160,6 +160,7 @@ def tile_picked_listsmooth_sigmoid_p_kernel(
             for e in range(2):
                 t = 2 * pair + e
                 nc.scalar.activation(z_planes[:, t, :], acc[:, e, :], ACT.Copy, scale=gk_sb[:, t : t + 1])
+        round_values(1)
         z_q = mx_pair("z_q")
         z_bf = [sb(f"z_bf{half}", [P, HALF, PACK], BF16) for half in range(2)]
         for u in range(2):
@@ -219,10 +220,13 @@ def tile_picked_listsmooth_sigmoid_p_kernel(
         interleave(zv_bf[:], zv_planes[:])
         gate(3, RANGES)
         quantize(zv_q, slice(0, N), zv_bf[:])
+        spare = bank(7, [P, N])
+        for number in range(4):
+            product(spare[:], zv_q, chunk(number), zv_q, slice(0, N))
         out_view = out.rearrange("(m p) v -> p m v", p=P)
         for lo, hi in RANGES:
             zp_bf = sb(f"zp_bf{lo}", [P, hi - lo, PACK], BF16)
-            interleave(zp_bf[:], zp_planes[:, :, lo:hi])
+            interleave(zp_bf[:], zp_planes[:, :, lo:hi], nc.vector.tensor_copy if lo == 0 else nc.scalar.copy)
             quantize(zp_q, slice(lo, hi), zp_bf[:])
         for lo, hi in RANGES:
             width = hi - lo

@@ -129,6 +129,9 @@ def tile_picked_listsmooth_sigmoid_p_kernel(
         w2_bf = round_dealt("w2", w2_raw)
         w2_q = mx_pair("w2_q")
         quantize(w2_q, slice(0, H), w2_bf[:])
+        early = bank(7, [P, H])
+        for number in range(3):
+            product(early[:], w2_q, chunk(number), w2_q, slice(0, H))
         nc.vector.tensor_copy(queries[0][:], x_wd[:].bitcast(U32).indirect(qs_sb[:]))
         nc.vector.tensor_copy(keys[0][:].rearrange("p (t m) -> p m t", t=PACK), x_wd[:].bitcast(U32).indirect(offs_sb[:]))
         w1_bf = round_dealt("w1", w1_raw)
@@ -179,14 +182,14 @@ def tile_picked_listsmooth_sigmoid_p_kernel(
                 acc = bank(u, [P, V])
                 product(acc[:], z_q, chunk(u), z2_q, slice(0, V))
                 nc.scalar.copy(windows[u][:], acc[:])
+                if u != 1:
+                    nc.sync.dma_start(plains[u][:], windows[u][:])
 
         scores(0)
         wv_q = mx_pair("wv_q")
         interleave(z_bf[1][:], z_planes[:])
         quantize(wv_q, slice(0, N), wv_bf[:])
         scores(1)
-        for u in range(2, PACK):
-            nc.sync.dma_start(plains[u][:], windows[u][:])
         zv_planes = sb("zv_planes", [P, PACK, N], BF16)
         for u in range(PACK):
             acc = bank(4 + u, [P, N])
@@ -196,9 +199,10 @@ def tile_picked_listsmooth_sigmoid_p_kernel(
         zp_planes = sb("zp_planes", [P, PACK, V], BF16)
         zp_q = mx_pair("zp_q")
 
+        gated = [sb(f"gated{u}", [P, V], F32) for u in range(PACK)]
+
         def gate(u, ranges):
             joined = sb(f"joined{u}", [P, V], F32)
-            gated = sb(f"gated{u}", [P, V], F32)
             for lo, hi in ranges:
                 for first in range(lo, hi, HALF):
                     last = min(first + HALF, hi)
@@ -208,12 +212,18 @@ def tile_picked_listsmooth_sigmoid_p_kernel(
                         plains[u][:, first:last],
                         ALU.add,
                     )
-                nc.scalar.activation(gated[:, lo:hi], joined[:, lo:hi], ACT.Sigmoid, scale=0.0625)
-                nc.scalar.activation(zp_planes[:, u, lo:hi], gated[:, lo:hi], ACT.Copy, scale=gt_sb[:, u : u + 1])
+                nc.scalar.activation(gated[u][:, lo:hi], joined[:, lo:hi], ACT.Sigmoid, scale=0.0625)
 
-        for u in range(2):
-            nc.vector.tensor_copy(plains[u][:], windows[u][:])
+        def weight_on_scalar(u, lo, hi):
+            nc.scalar.activation(zp_planes[:, u, lo:hi], gated[u][:, lo:hi], ACT.Copy, scale=gt_sb[:, u : u + 1])
+
+        def weight_on_vector(u, lo, hi):
+            nc.vector.tensor_scalar(zp_planes[:, u, lo:hi], gated[u][:, lo:hi], gt_sb[:, u : u + 1], None, ALU.mult)
+
+        nc.vector.tensor_copy(plains[1][:], windows[1][:])
+        for u in (1, 0):
             gate(u, ((0, V),))
+            weight_on_scalar(u, 0, V)
         gate(2, ((0, V),))
         zv_bf = sb("zv_bf", [P, N, PACK], BF16)
         zv_q = mx_pair("zv_q")
@@ -221,8 +231,13 @@ def tile_picked_listsmooth_sigmoid_p_kernel(
         gate(3, RANGES)
         quantize(zv_q, slice(0, N), zv_bf[:])
         spare = bank(7, [P, N])
-        for number in range(4):
+        for number in range(2):
             product(spare[:], zv_q, chunk(number), zv_q, slice(0, N))
+        for u in (2, 3):
+            weight_on_vector(u, 0, HALF)
+        weight_on_scalar(2, HALF, V)
+        for lo, hi in RANGES[1:]:
+            weight_on_scalar(3, lo, hi)
         out_view = out.rearrange("(m p) v -> p m v", p=P)
         for lo, hi in RANGES:
             zp_bf = sb(f"zp_bf{lo}", [P, hi - lo, PACK], BF16)

@@ -154,7 +154,8 @@ def tile_picked_listsmooth_sigmoid_p_kernel(
                 wv_raw[part][:].rearrange("p j (c r) -> p c j r", r=4),
             )
 
-        round_values(0)
+        for part in range(2):
+            round_values(part)
         z_planes = sb("z_planes", [P, PACK, HALF], BF16)
         for pair in range(2):
             acc = bank(4 + pair, [P, 2, HALF])
@@ -163,7 +164,6 @@ def tile_picked_listsmooth_sigmoid_p_kernel(
             for e in range(2):
                 t = 2 * pair + e
                 nc.scalar.activation(z_planes[:, t, :], acc[:, e, :], ACT.Copy, scale=gk_sb[:, t : t + 1])
-        round_values(1)
         z_q = mx_pair("z_q")
         z_bf = [sb(f"z_bf{half}", [P, HALF, PACK], BF16) for half in range(2)]
         for u in range(2):
@@ -171,7 +171,18 @@ def tile_picked_listsmooth_sigmoid_p_kernel(
             for t in range(PACK):
                 product(acc[:, t, :], w1_q, chunk(t), keys, chunk(u))
             weighted_read(z_bf[0][:, chunk(u), :], acc, gk_sb)
+        wv_q = mx_pair("wv_q")
+        quantize(wv_q, slice(0, N), wv_bf[:])
         quantize(z2_q, slice(0, V), z2_bf[:])
+        zv_planes = sb("zv_planes", [P, PACK, N], BF16)
+
+        def values(u):
+            acc = bank(4 + u, [P, N])
+            product(acc[:], keys, chunk(u), wv_q, slice(0, N))
+            nc.scalar.activation(zv_planes[:, u, :], acc[:], ACT.Copy, scale=gi_sb[:, u : u + 1])
+
+        for u in range(2):
+            values(u)
 
         windows = [sb(f"window{u}", [P, V], F32) for u in range(PACK)]
         plains = [sb(f"plain{u}", [P, V], F32) for u in range(PACK)]
@@ -186,15 +197,12 @@ def tile_picked_listsmooth_sigmoid_p_kernel(
                     nc.sync.dma_start(plains[u][:], windows[u][:])
 
         scores(0)
-        wv_q = mx_pair("wv_q")
         interleave(z_bf[1][:], z_planes[:])
-        quantize(wv_q, slice(0, N), wv_bf[:])
         scores(1)
-        zv_planes = sb("zv_planes", [P, PACK, N], BF16)
-        for u in range(PACK):
-            acc = bank(4 + u, [P, N])
-            product(acc[:], keys, chunk(u), wv_q, slice(0, N))
-            nc.scalar.activation(zv_planes[:, u, :], acc[:], ACT.Copy, scale=gi_sb[:, u : u + 1])
+        for u in range(2, PACK):
+            values(u)
+        zv_bf = sb("zv_bf", [P, N, PACK], BF16)
+        interleave(zv_bf[:, 384:, :], zv_planes[:, :, 384:], nc.scalar.copy)
 
         zp_planes = sb("zp_planes", [P, PACK, V], BF16)
         zp_q = mx_pair("zp_q")
@@ -225,11 +233,10 @@ def tile_picked_listsmooth_sigmoid_p_kernel(
             gate(u, ((0, V),))
             weight_on_scalar(u, 0, V)
         gate(2, ((0, V),))
-        zv_bf = sb("zv_bf", [P, N, PACK], BF16)
-        zv_q = mx_pair("zv_q")
-        interleave(zv_bf[:], zv_planes[:])
-        gate(3, RANGES)
+        zv_q = (sb("zv_wd", [P, N], U32, "plain2"), sb("zv_sc", [P, N], U8))
+        interleave(zv_bf[:, :384, :], zv_planes[:, :, :384])
         quantize(zv_q, slice(0, N), zv_bf[:])
+        gate(3, RANGES)
         spare = bank(7, [P, N])
         for number in range(2):
             product(spare[:], zv_q, chunk(number), zv_q, slice(0, N))
@@ -243,14 +250,24 @@ def tile_picked_listsmooth_sigmoid_p_kernel(
             zp_bf = sb(f"zp_bf{lo}", [P, hi - lo, PACK], BF16)
             interleave(zp_bf[:], zp_planes[:, :, lo:hi], nc.vector.tensor_copy if lo == 0 else nc.scalar.copy)
             quantize(zp_q, slice(lo, hi), zp_bf[:])
-        for lo, hi in RANGES:
-            width = hi - lo
-            rows = 512 // width
-            for m0 in range(0, PACK, rows):
-                number = lo // P + m0 // rows
-                acc = bank(number, [P, rows, width])
-                for m in range(rows):
-                    product(acc[:, m, :], zv_q, chunk(m0 + m), zp_q, slice(lo, hi))
-                result = sb(f"result{number}", [P, rows, width], F32)
-                nc.vector.scalar_tensor_tensor(result[:], acc[:], 0.0625, res_sb[:, m0 : m0 + rows, lo:hi], ALU.mult, ALU.add)
-                nc.sync.dma_start(out_view[:, m0 : m0 + rows, lo:hi], result[:])
+
+        def result(number, m0, rows, lo, hi, shared):
+            acc = bank(number, [P, rows, hi - lo])
+            for m in range(rows):
+                product(acc[:, m, :], zv_q, chunk(m0 + m), zp_q, slice(lo, hi))
+            tile = sb(f"result{number}", [P, rows, hi - lo], F32)
+            if shared:
+                scaled = sb("scaled", [P, rows, hi - lo], F32)
+                nc.scalar.activation(scaled[:], acc[:], ACT.Copy, scale=0.0625)
+                nc.gpsimd.tensor_tensor(tile[:], scaled[:], res_sb[:, m0 : m0 + rows, lo:hi], ALU.add)
+            else:
+                nc.vector.scalar_tensor_tensor(tile[:], acc[:], 0.0625, res_sb[:, m0 : m0 + rows, lo:hi], ALU.mult, ALU.add)
+            queue = nc.scalar if shared else nc.sync
+            queue.dma_start(out_view[:, m0 : m0 + rows, lo:hi], tile[:])
+
+        result(0, 0, 1, 0, 256, False)
+        result(5, 1, 1, 0, 256, False)
+        result(1, 2, 2, 0, 256, False)
+        result(2, 0, 2, 256, 384, True)
+        result(3, 0, 4, 384, 512, False)
+        result(4, 2, 2, 256, 384, False)

@@ -251,23 +251,17 @@ def tile_picked_listsmooth_sigmoid_p_kernel(
             interleave(zp_bf[:], zp_planes[:, :, lo:hi], nc.vector.tensor_copy if lo == 0 else nc.scalar.copy)
             quantize(zp_q, slice(lo, hi), zp_bf[:])
 
-        def result(number, m0, rows, lo, hi, shared):
+        def result(number, m0, rows, lo, hi):
             acc = bank(number, [P, rows, hi - lo])
             for m in range(rows):
                 product(acc[:, m, :], zv_q, chunk(m0 + m), zp_q, slice(lo, hi))
             tile = sb(f"result{number}", [P, rows, hi - lo], F32)
-            if shared:
-                scaled = sb("scaled", [P, rows, hi - lo], F32)
-                nc.scalar.activation(scaled[:], acc[:], ACT.Copy, scale=0.0625)
-                nc.gpsimd.tensor_tensor(tile[:], scaled[:], res_sb[:, m0 : m0 + rows, lo:hi], ALU.add)
-            else:
-                nc.vector.scalar_tensor_tensor(tile[:], acc[:], 0.0625, res_sb[:, m0 : m0 + rows, lo:hi], ALU.mult, ALU.add)
-            queue = nc.scalar if shared else nc.sync
-            queue.dma_start(out_view[:, m0 : m0 + rows, lo:hi], tile[:])
+            nc.vector.scalar_tensor_tensor(tile[:], acc[:], 0.0625, res_sb[:, m0 : m0 + rows, lo:hi], ALU.mult, ALU.add)
+            nc.sync.dma_start(out_view[:, m0 : m0 + rows, lo:hi], tile[:])
 
-        result(0, 0, 1, 0, 256, False)
-        result(5, 1, 1, 0, 256, False)
-        result(1, 2, 2, 0, 256, False)
-        result(2, 0, 2, 256, 384, True)
-        result(3, 0, 4, 384, 512, False)
-        result(4, 2, 2, 256, 384, False)
+        result(0, 0, 1, 0, 256)
+        result(5, 1, 1, 0, 256)
+        result(1, 2, 2, 0, 256)
+        result(2, 0, 4, 256, 384)
+        result(3, 0, 2, 384, 512)
+        result(4, 2, 2, 384, 512)

@@ -141,7 +141,7 @@ def tile_picked_listsmooth_sigmoid_p_kernel(
         z2_bf = sb("z2_bf", [P, V, PACK], BF16)
         z2_q = mx_pair("z2_q")
         for c in range(4):
-            acc = bank(c, [P, PACK, P])
+            acc = bank(c % 2, [P, PACK, P])
             for t in range(PACK):
                 product(acc[:, t, :], w2_q, chunk(t), queries, chunk(c))
             weighted_read(z2_bf[:, chunk(c), :], acc, gq_sb)
@@ -184,17 +184,18 @@ def tile_picked_listsmooth_sigmoid_p_kernel(
         for u in range(2):
             values(u)
 
-        windows = [sb(f"window{u}", [P, V], F32) for u in range(PACK)]
-        plains = [sb(f"plain{u}", [P, V], F32) for u in range(PACK)]
+        windows = [sb(f"window{u}", [P, V if u == 3 else 2 * V], F32) for u in range(PACK)]
+        nc.vector.memset(windows[1][:, V:], 0.0)
+        plains = [windows[2][:, V:], windows[0][:, V:]] + [sb(f"plain{u}", [P, V], F32)[:] for u in (2, 3)]
 
         def scores(half):
             quantize(z_q, slice(HALF * half, HALF * (half + 1)), z_bf[half][:])
             for u in range(2 * half, 2 * half + 2):
                 acc = bank(u, [P, V])
                 product(acc[:], z_q, chunk(u), z2_q, slice(0, V))
-                nc.scalar.copy(windows[u][:], acc[:])
+                nc.scalar.copy(windows[u][:, :V], acc[:])
                 if u != 1:
-                    nc.sync.dma_start(plains[u][:], windows[u][:])
+                    nc.sync.dma_start(plains[u], windows[u][:, :V])
 
         scores(0)
         interleave(z_bf[1][:], z_planes[:])
@@ -207,31 +208,23 @@ def tile_picked_listsmooth_sigmoid_p_kernel(
         zp_planes = sb("zp_planes", [P, PACK, V], BF16)
         zp_q = mx_pair("zp_q")
 
-        gated = [sb(f"gated{u}", [P, V], F32) for u in range(PACK)]
+        gated = sb("gated", [P, PACK, V], F32)
 
         def gate(u, ranges):
             joined = sb(f"joined{u}", [P, V], F32)
             for lo, hi in ranges:
-                for first in range(lo, hi, HALF):
-                    last = min(first + HALF, hi)
-                    nc.vector.tensor_tensor(
-                        joined[:, first:last],
-                        windows[u][:].indirect(nb_sb[:, first // 16 : last // 16]),
-                        plains[u][:, first:last],
-                        ALU.add,
-                    )
-                nc.scalar.activation(gated[u][:, lo:hi], joined[:, lo:hi], ACT.Sigmoid, scale=0.0625)
+                nc.vector.tensor_tensor(
+                    joined[:, lo:hi], windows[u][:].indirect(nb_sb[:, lo // 16 : hi // 16]), plains[u][:, lo:hi], ALU.add
+                )
+                nc.scalar.activation(gated[:, u, lo:hi], joined[:, lo:hi], ACT.Sigmoid, scale=0.0625)
 
         def weight_on_scalar(u, lo, hi):
-            nc.scalar.activation(zp_planes[:, u, lo:hi], gated[u][:, lo:hi], ACT.Copy, scale=gt_sb[:, u : u + 1])
+            nc.scalar.activation(zp_planes[:, u, lo:hi], gated[:, u, lo:hi], ACT.Copy, scale=gt_sb[:, u : u + 1])
 
-        def weight_on_vector(u, lo, hi):
-            nc.vector.tensor_scalar(zp_planes[:, u, lo:hi], gated[u][:, lo:hi], gt_sb[:, u : u + 1], None, ALU.mult)
-
-        nc.vector.tensor_copy(plains[1][:], windows[1][:])
+        nc.vector.tensor_copy(plains[1], windows[1][:, :V])
         for u in (1, 0):
             gate(u, ((0, V),))
-            weight_on_scalar(u, 0, V)
+            weight_on_scalar(u, HALF, V)
         gate(2, ((0, V),))
         zv_q = (sb("zv_wd", [P, N], U32, "plain2"), sb("zv_sc", [P, N], U8))
         interleave(zv_bf[:, :384, :], zv_planes[:, :, :384])
@@ -240,15 +233,21 @@ def tile_picked_listsmooth_sigmoid_p_kernel(
         spare = bank(7, [P, N])
         for number in range(2):
             product(spare[:], zv_q, chunk(number), zv_q, slice(0, N))
-        for u in (2, 3):
-            weight_on_vector(u, 0, HALF)
         weight_on_scalar(2, HALF, V)
         for lo, hi in RANGES[1:]:
             weight_on_scalar(3, lo, hi)
         out_view = out.rearrange("(m p) v -> p m v", p=P)
         for lo, hi in RANGES:
             zp_bf = sb(f"zp_bf{lo}", [P, hi - lo, PACK], BF16)
-            interleave(zp_bf[:], zp_planes[:, :, lo:hi], nc.vector.tensor_copy if lo == 0 else nc.scalar.copy)
+            if lo == 0:
+                nc.vector.tensor_tensor(
+                    zp_bf[:].rearrange("p (c i) t -> p c t i", i=4),
+                    gated[:, :, lo:hi].rearrange("p t (c i) -> p c t i", i=4),
+                    gt_sb[:].unsqueeze(1).unsqueeze(3).to_broadcast([P, HALF // 4, PACK, 4]),
+                    ALU.mult,
+                )
+            else:
+                interleave(zp_bf[:], zp_planes[:, :, lo:hi], nc.scalar.copy)
             quantize(zp_q, slice(lo, hi), zp_bf[:])
 
         def result(number, m0, rows, lo, hi):

@@ -130,7 +130,7 @@ def tile_picked_listsmooth_sigmoid_p_kernel(
         w2_q = mx_pair("w2_q")
         quantize(w2_q, slice(0, H), w2_bf[:])
         early = bank(7, [P, H])
-        for number in range(3):
+        for number in range(1):
             product(early[:], w2_q, chunk(number), w2_q, slice(0, H))
         nc.vector.tensor_copy(queries[0][:], x_wd[:].bitcast(U32).indirect(qs_sb[:]))
         nc.vector.tensor_copy(keys[0][:].rearrange("p (t m) -> p m t", t=PACK), x_wd[:].bitcast(U32).indirect(offs_sb[:]))
@@ -156,14 +156,12 @@ def tile_picked_listsmooth_sigmoid_p_kernel(
 
         for part in range(2):
             round_values(part)
-        z_planes = sb("z_planes", [P, PACK, HALF], BF16)
-        for pair in range(2):
-            acc = bank(4 + pair, [P, 2, HALF])
-            for e in range(2):
-                product(acc[:, e, :], w1_q, chunk(2 * pair + e), keys, slice(HALF, S))
-            for e in range(2):
-                t = 2 * pair + e
-                nc.scalar.activation(z_planes[:, t, :], acc[:, e, :], ACT.Copy, scale=gk_sb[:, t : t + 1])
+        z_planes = sb("z_planes", [P, PACK, P], BF16)
+        acc = bank(4, [P, PACK, P])
+        for t in range(PACK):
+            product(acc[:, t, :], w1_q, chunk(t), keys, chunk(3))
+        for t in range(PACK):
+            nc.scalar.activation(z_planes[:, t, :], acc[:, t, :], ACT.Copy, scale=gk_sb[:, t : t + 1])
         z_q = mx_pair("z_q")
         z_bf = [sb(f"z_bf{half}", [P, HALF, PACK], BF16) for half in range(2)]
         for u in range(2):
@@ -198,7 +196,11 @@ def tile_picked_listsmooth_sigmoid_p_kernel(
                     nc.sync.dma_start(plains[u], windows[u][:, :V])
 
         scores(0)
-        interleave(z_bf[1][:], z_planes[:])
+        acc = bank(2, [P, PACK, P])
+        for t in range(PACK):
+            product(acc[:, t, :], w1_q, chunk(t), keys, chunk(2))
+        weighted_read(z_bf[1][:, chunk(0), :], acc, gk_sb)
+        interleave(z_bf[1][:, chunk(1), :], z_planes[:])
         scores(1)
         for u in range(2, PACK):
             values(u)
@@ -231,19 +233,20 @@ def tile_picked_listsmooth_sigmoid_p_kernel(
         quantize(zv_q, slice(0, N), zv_bf[:])
         gate(3, RANGES)
         spare = bank(7, [P, N])
-        for number in range(2):
+        for number in range(4):
             product(spare[:], zv_q, chunk(number), zv_q, slice(0, N))
         weight_on_scalar(2, HALF, V)
         for lo, hi in RANGES[1:]:
             weight_on_scalar(3, lo, hi)
         out_view = out.rearrange("(m p) v -> p m v", p=P)
-        for lo, hi in RANGES:
+        for lo in range(0, V, P):
+            hi = lo + P
             zp_bf = sb(f"zp_bf{lo}", [P, hi - lo, PACK], BF16)
-            if lo == 0:
+            if lo < HALF:
                 nc.vector.tensor_tensor(
                     zp_bf[:].rearrange("p (c i) t -> p c t i", i=4),
                     gated[:, :, lo:hi].rearrange("p t (c i) -> p c t i", i=4),
-                    gt_sb[:].unsqueeze(1).unsqueeze(3).to_broadcast([P, HALF // 4, PACK, 4]),
+                    gt_sb[:].unsqueeze(1).unsqueeze(3).to_broadcast([P, P // 4, PACK, 4]),
                     ALU.mult,
                 )
             else:
@@ -258,9 +261,9 @@ def tile_picked_listsmooth_sigmoid_p_kernel(
             nc.vector.scalar_tensor_tensor(tile[:], acc[:], 0.0625, res_sb[:, m0 : m0 + rows, lo:hi], ALU.mult, ALU.add)
             nc.sync.dma_start(out_view[:, m0 : m0 + rows, lo:hi], tile[:])
 
-        result(0, 0, 1, 0, 256)
-        result(5, 1, 1, 0, 256)
-        result(1, 2, 2, 0, 256)
+        result(0, 0, 2, 0, 128)
+        result(5, 2, 2, 0, 128)
+        result(1, 0, 4, 128, 256)
         result(2, 0, 4, 256, 384)
         result(3, 0, 2, 384, 512)
         result(4, 2, 2, 384, 512)

@@ -261,9 +261,9 @@ def tile_picked_listsmooth_sigmoid_p_kernel(
             nc.vector.scalar_tensor_tensor(tile[:], acc[:], 0.0625, res_sb[:, m0 : m0 + rows, lo:hi], ALU.mult, ALU.add)
             nc.sync.dma_start(out_view[:, m0 : m0 + rows, lo:hi], tile[:])
 
-        result(0, 0, 2, 0, 128)
-        result(5, 2, 2, 0, 128)
+        result(0, 0, 1, 0, 128)
+        result(5, 1, 3, 0, 128)
         result(1, 0, 4, 128, 256)
         result(2, 0, 4, 256, 384)
-        result(3, 0, 2, 384, 512)
-        result(4, 2, 2, 384, 512)
+        result(3, 0, 3, 384, 512)
+        result(4, 3, 1, 384, 512)

@@ -120,19 +120,16 @@ def tile_picked_listsmooth_sigmoid_p_kernel(
 
         keys = mx_pair("key")
         queries = mx_pair("query")
-        key_sc_listed = sb("key_sc_listed", [P, S], U8)
         nc.vector.tensor_copy(queries[1][:], x_sc[:].indirect(qs_sb[:]))
-        nc.vector.tensor_copy(key_sc_listed[:], x_sc[:].indirect(offs_sb[:]))
-        nc.vector.tensor_copy(
-            keys[1][:].rearrange("p (t m) -> p m t", t=PACK), key_sc_listed[:].rearrange("p (m t) -> p m t", t=PACK)
-        )
+        nc.vector.tensor_copy(keys[1][:].rearrange("p (t m) -> p m t", t=PACK), x_sc[:].indirect(offs_sb[:]))
         w2_bf = round_dealt("w2", w2_raw)
         w2_q = mx_pair("w2_q")
         quantize(w2_q, slice(0, H), w2_bf[:])
-        early = bank(7, [P, H])
-        for number in range(1):
-            product(early[:], w2_q, chunk(number), w2_q, slice(0, H))
-        nc.vector.tensor_copy(queries[0][:], x_wd[:].bitcast(U32).indirect(qs_sb[:]))
+        for part in range(2):
+            nc.vector.tensor_copy(
+                queries[0][:, HALF * part : HALF * (part + 1)],
+                x_wd[:].bitcast(U32).indirect(qs_sb[:, 16 * part : 16 * (part + 1)]),
+            )
         nc.vector.tensor_copy(keys[0][:].rearrange("p (t m) -> p m t", t=PACK), x_wd[:].bitcast(U32).indirect(offs_sb[:]))
         w1_bf = round_dealt("w1", w1_raw)
         w1_q = mx_pair("w1_q")
@@ -233,7 +230,7 @@ def tile_picked_listsmooth_sigmoid_p_kernel(
         quantize(zv_q, slice(0, N), zv_bf[:])
         gate(3, RANGES)
         spare = bank(7, [P, N])
-        for number in range(4):
+        for number in range(2):
             product(spare[:], zv_q, chunk(number), zv_q, slice(0, N))
         weight_on_scalar(2, HALF, V)
         for lo, hi in RANGES[1:]:

@@ -60,7 +60,7 @@ def tile_picked_listsmooth_sigmoid_p_kernel(
         warm = sb("warm", [P, 1], F32)
         qs_sb = load_list("qs_sb", qs)
         offs_sb = load_list("offs_sb", offs)
-        for q, queue in enumerate((nc.scalar, nc.scalar, nc.sync, nc.sync)):
+        for q, queue in enumerate((nc.scalar, nc.scalar, nc.scalar, nc.sync)):
             queue.dma_start(sc_rows[32 * q : 32 * q + 4, :], x_scales[0, 4 * q : 4 * q + 4, :].bitcast(I32))
         nc.gpsimd.memset(cold[:], 0.0)
         nc.scalar.activation(warm[:], cold[:], ACT.Sigmoid)
@@ -70,10 +70,10 @@ def tile_picked_listsmooth_sigmoid_p_kernel(
         w2_raw = [sb(f"w2_raw{part}", [P, PACK, HALF], F32) for part in range(2)]
         load_halves(w2_raw, w2)
         nc.sync.dma_start(x_wd[:], x_words[0].rearrange("p c r -> p (c r)").bitcast(I32))
-        w1_raw = [sb(f"w1_raw{part}", [P, PACK, HALF], F32) for part in range(2)]
-        load_halves(w1_raw, w1)
         gq_sb = load_gain("gq_sb", gq)
         gk_sb = load_gain("gk_sb", gk)
+        w1_raw = [sb(f"w1_raw{part}", [P, PACK, HALF], F32) for part in range(2)]
+        load_halves(w1_raw, w1)
         wv_raw = [sb(f"wv_raw{part}", [P, PACK, HALF], F32) for part in range(2)]
         load_halves(wv_raw, wv)
         nb_sb = load_list("nb_sb", nb)
@@ -135,13 +135,13 @@ def tile_picked_listsmooth_sigmoid_p_kernel(
         w1_q = mx_pair("w1_q")
         quantize(w1_q, slice(0, H), w1_bf[:])
 
-        z2_bf = sb("z2_bf", [P, V, PACK], BF16)
+        z2_bf = [sb("z2_bf0", [P, HALF, PACK], BF16), sb("z2_bf1", [P, HALF, PACK], BF16, "w1_raw1")]
         z2_q = mx_pair("z2_q")
         for c in range(4):
             acc = bank(c % 2, [P, PACK, P])
             for t in range(PACK):
                 product(acc[:, t, :], w2_q, chunk(t), queries, chunk(c))
-            weighted_read(z2_bf[:, chunk(c), :], acc, gq_sb)
+            weighted_read(z2_bf[c // 2][:, chunk(c % 2), :], acc, gq_sb)
 
         wv_bf = sb("wv_bf", [P, N, PACK], BF16)
 
@@ -161,14 +161,15 @@ def tile_picked_listsmooth_sigmoid_p_kernel(
             nc.scalar.activation(z_planes[:, t, :], acc[:, t, :], ACT.Copy, scale=gk_sb[:, t : t + 1])
         z_q = mx_pair("z_q")
         z_bf = [sb(f"z_bf{half}", [P, HALF, PACK], BF16) for half in range(2)]
+        interleave(z_bf[1][:, chunk(1), :], z_planes[:], nc.scalar.copy)
         for u in range(2):
             acc = bank(6 + u, [P, PACK, P])
             for t in range(PACK):
                 product(acc[:, t, :], w1_q, chunk(t), keys, chunk(u))
             weighted_read(z_bf[0][:, chunk(u), :], acc, gk_sb)
         wv_q = mx_pair("wv_q")
-        quantize(wv_q, slice(0, N), wv_bf[:])
-        quantize(z2_q, slice(0, V), z2_bf[:])
+        for part in range(2):
+            quantize(z2_q, slice(HALF * part, HALF * (part + 1)), z2_bf[part][:])
         zv_planes = sb("zv_planes", [P, PACK, N], BF16)
 
         def values(u):
@@ -176,30 +177,30 @@ def tile_picked_listsmooth_sigmoid_p_kernel(
             product(acc[:], keys, chunk(u), wv_q, slice(0, N))
             nc.scalar.activation(zv_planes[:, u, :], acc[:], ACT.Copy, scale=gi_sb[:, u : u + 1])
 
-        for u in range(2):
-            values(u)
-
         windows = [sb(f"window{u}", [P, V if u == 3 else 2 * V], F32) for u in range(PACK)]
         nc.vector.memset(windows[1][:, V:], 0.0)
         plains = [windows[2][:, V:], windows[0][:, V:]] + [sb(f"plain{u}", [P, V], F32)[:] for u in (2, 3)]
 
-        def scores(half):
-            quantize(z_q, slice(HALF * half, HALF * (half + 1)), z_bf[half][:])
-            for u in range(2 * half, 2 * half + 2):
-                acc = bank(u, [P, V])
-                product(acc[:], z_q, chunk(u), z2_q, slice(0, V))
-                nc.scalar.copy(windows[u][:, :V], acc[:])
-                if u != 1:
-                    nc.sync.dma_start(plains[u], windows[u][:, :V])
+        def scores(u):
+            acc = bank(u, [P, V])
+            product(acc[:], z_q, chunk(u), z2_q, slice(0, V))
+            nc.scalar.copy(windows[u][:, :V], acc[:])
+            if u != 1:
+                nc.sync.dma_start(plains[u], windows[u][:, :V])
 
-        scores(0)
+        for u in range(2):
+            quantize(z_q, chunk(u), z_bf[0][:, chunk(u), :])
+            scores(u)
+        quantize(wv_q, slice(0, N), wv_bf[:])
+        values(0)
         acc = bank(2, [P, PACK, P])
         for t in range(PACK):
             product(acc[:, t, :], w1_q, chunk(t), keys, chunk(2))
         weighted_read(z_bf[1][:, chunk(0), :], acc, gk_sb)
-        interleave(z_bf[1][:, chunk(1), :], z_planes[:])
-        scores(1)
+        quantize(z_q, slice(HALF, S), z_bf[1][:])
         for u in range(2, PACK):
+            scores(u)
+        for u in range(1, PACK):
             values(u)
         zv_bf = sb("zv_bf", [P, N, PACK], BF16)
         interleave(zv_bf[:, 384:, :], zv_planes[:, :, 384:], nc.scalar.copy)

@@ -153,23 +153,20 @@ def tile_picked_listsmooth_sigmoid_p_kernel(
 
         for part in range(2):
             round_values(part)
-        z_planes = sb("z_planes", [P, PACK, P], BF16)
-        acc = bank(4, [P, PACK, P])
-        for t in range(PACK):
-            product(acc[:, t, :], w1_q, chunk(t), keys, chunk(3))
-        for t in range(PACK):
-            nc.scalar.activation(z_planes[:, t, :], acc[:, t, :], ACT.Copy, scale=gk_sb[:, t : t + 1])
         z_q = mx_pair("z_q")
-        z_bf = [sb(f"z_bf{half}", [P, HALF, PACK], BF16) for half in range(2)]
-        interleave(z_bf[1][:, chunk(1), :], z_planes[:], nc.scalar.copy)
-        for u in range(2):
-            acc = bank(6 + u, [P, PACK, P])
+        z_bf = [sb(f"z_bf{u}", [P, P, PACK], BF16) for u in range(PACK)]
+
+        def key_products(u, number):
+            acc = bank(number, [P, PACK, P])
             for t in range(PACK):
                 product(acc[:, t, :], w1_q, chunk(t), keys, chunk(u))
-            weighted_read(z_bf[0][:, chunk(u), :], acc, gk_sb)
+            return acc
+
+        z_planes = sb("z_planes", [P, PACK, P], BF16)
+        acc = key_products(3, 4)
+        for t in range(PACK):
+            nc.scalar.activation(z_planes[:, t, :], acc[:, t, :], ACT.Copy, scale=gk_sb[:, t : t + 1])
         wv_q = mx_pair("wv_q")
-        for part in range(2):
-            quantize(z2_q, slice(HALF * part, HALF * (part + 1)), z2_bf[part][:])
         zv_planes = sb("zv_planes", [P, PACK, N], BF16)
 
         def values(u):
@@ -177,33 +174,33 @@ def tile_picked_listsmooth_sigmoid_p_kernel(
             product(acc[:], keys, chunk(u), wv_q, slice(0, N))
             nc.scalar.activation(zv_planes[:, u, :], acc[:], ACT.Copy, scale=gi_sb[:, u : u + 1])
 
-        windows = [sb(f"window{u}", [P, V if u == 3 else 2 * V], F32) for u in range(PACK)]
+        windows = [sb(f"window{u}", [P, V if u == 2 else 2 * V], F32) for u in range(PACK)]
         nc.vector.memset(windows[1][:, V:], 0.0)
-        plains = [windows[2][:, V:], windows[0][:, V:]] + [sb(f"plain{u}", [P, V], F32)[:] for u in (2, 3)]
+        plains = [windows[3][:, V:], windows[0][:, V:]] + [sb(f"plain{u}", [P, V], F32)[:] for u in (2, 3)]
 
         def scores(u):
+            quantize(z_q, chunk(u), z_bf[u][:])
             acc = bank(u, [P, V])
             product(acc[:], z_q, chunk(u), z2_q, slice(0, V))
             nc.scalar.copy(windows[u][:, :V], acc[:])
             if u != 1:
                 nc.sync.dma_start(plains[u], windows[u][:, :V])
 
-        for u in range(2):
-            quantize(z_q, chunk(u), z_bf[0][:, chunk(u), :])
-            scores(u)
+        weighted_read(z_bf[0][:], key_products(0, 6), gk_sb)
+        for part in range(2):
+            quantize(z2_q, slice(HALF * part, HALF * (part + 1)), z2_bf[part][:])
+        scores(0)
+        weighted_read(z_bf[1][:], key_products(1, 7), gk_sb)
+        interleave(z_bf[3][:], z_planes[:])
+        scores(1)
+        scores(3)
+        weighted_read(z_bf[2][:], key_products(2, 5), gk_sb)
         quantize(wv_q, slice(0, N), wv_bf[:])
-        values(0)
-        acc = bank(2, [P, PACK, P])
-        for t in range(PACK):
-            product(acc[:, t, :], w1_q, chunk(t), keys, chunk(2))
-        weighted_read(z_bf[1][:, chunk(0), :], acc, gk_sb)
-        quantize(z_q, slice(HALF, S), z_bf[1][:])
-        for u in range(2, PACK):
-            scores(u)
-        for u in range(1, PACK):
+        scores(2)
+        for u in range(PACK):
             values(u)
         zv_bf = sb("zv_bf", [P, N, PACK], BF16)
-        interleave(zv_bf[:, 384:, :], zv_planes[:, :, 384:], nc.scalar.copy)
+        interleave(zv_bf[:, HALF:, :], zv_planes[:, :, HALF:], nc.scalar.copy)
 
         zp_planes = sb("zp_planes", [P, PACK, V], BF16)
         zp_q = mx_pair("zp_q")
@@ -225,17 +222,17 @@ def tile_picked_listsmooth_sigmoid_p_kernel(
         for u in (1, 0):
             gate(u, ((0, V),))
             weight_on_scalar(u, HALF, V)
-        gate(2, ((0, V),))
-        zv_q = (sb("zv_wd", [P, N], U32, "plain2"), sb("zv_sc", [P, N], U8))
-        interleave(zv_bf[:, :384, :], zv_planes[:, :, :384])
+        gate(3, ((0, V),))
+        zv_q = (sb("zv_wd", [P, N], U32, "plain3"), sb("zv_sc", [P, N], U8))
+        interleave(zv_bf[:, :HALF, :], zv_planes[:, :, :HALF])
         quantize(zv_q, slice(0, N), zv_bf[:])
-        gate(3, RANGES)
+        gate(2, RANGES)
         spare = bank(7, [P, N])
         for number in range(2):
             product(spare[:], zv_q, chunk(number), zv_q, slice(0, N))
-        weight_on_scalar(2, HALF, V)
+        weight_on_scalar(3, HALF, V)
         for lo, hi in RANGES[1:]:
-            weight_on_scalar(3, lo, hi)
+            weight_on_scalar(2, lo, hi)
         out_view = out.rearrange("(m p) v -> p m v", p=P)
         for lo in range(0, V, P):
             hi = lo + P
@@ -263,5 +260,6 @@ def tile_picked_listsmooth_sigmoid_p_kernel(
         result(5, 1, 3, 0, 128)
         result(1, 0, 4, 128, 256)
         result(2, 0, 4, 256, 384)
-        result(3, 0, 3, 384, 512)
-        result(4, 3, 1, 384, 512)
+        result(3, 0, 2, 384, 512)
+        result(4, 2, 1, 384, 512)
+        result(6, 3, 1, 384, 512)

@@ -133,26 +133,25 @@ def tile_picked_listsmooth_sigmoid_p_kernel(
         nc.vector.tensor_copy(keys[0][:].rearrange("p (t m) -> p m t", t=PACK), x_wd[:].bitcast(U32).indirect(offs_sb[:]))
         w1_bf = round_dealt("w1", w1_raw)
         w1_q = mx_pair("w1_q")
-        quantize(w1_q, slice(0, H), w1_bf[:])
 
-        z2_bf = [sb("z2_bf0", [P, HALF, PACK], BF16), sb("z2_bf1", [P, HALF, PACK], BF16, "w1_raw1")]
-        z2_q = mx_pair("z2_q")
-        for c in range(4):
-            acc = bank(c % 2, [P, PACK, P])
+        z2_bf = [sb("z2_bf0", [P, 384, PACK], BF16), sb("z2_bf1", [P, P, PACK], BF16, "w1_raw1")]
+
+        def read_queries(c):
+            acc = bank(c, [P, PACK, P])
             for t in range(PACK):
                 product(acc[:, t, :], w2_q, chunk(t), queries, chunk(c))
-            weighted_read(z2_bf[c // 2][:, chunk(c % 2), :], acc, gq_sb)
+            weighted_read(z2_bf[c // 3][:, chunk(c % 3), :], acc, gq_sb)
+
+        for c in range(3):
+            read_queries(c)
+        quantize(w1_q, slice(0, H), w1_bf[:])
+        read_queries(3)
+        z2_q = (sb("z2_wd", [P, V], U32, "w1_bf"), sb("z2_sc", [P, V], U8))
+        quantize(z2_q, slice(0, 384), z2_bf[0][:])
 
         wv_bf = sb("wv_bf", [P, N, PACK], BF16)
-
-        def round_values(part):
-            nc.scalar.copy(
-                wv_bf[:, HALF * part : HALF * (part + 1), :].rearrange("p (c r) j -> p c j r", r=4),
-                wv_raw[part][:].rearrange("p j (c r) -> p c j r", r=4),
-            )
-
-        for part in range(2):
-            round_values(part)
+        interleave(wv_bf[:, :HALF, :], wv_raw[0][:], nc.scalar.copy)
+        interleave(wv_bf[:, HALF:384, :], wv_raw[1][:, :, :P], nc.scalar.copy)
         z_q = mx_pair("z_q")
         z_bf = [sb(f"z_bf{u}", [P, P, PACK], BF16) for u in range(PACK)]
 
@@ -162,10 +161,12 @@ def tile_picked_listsmooth_sigmoid_p_kernel(
                 product(acc[:, t, :], w1_q, chunk(t), keys, chunk(u))
             return acc
 
+        first_keys = key_products(0, 6)
         z_planes = sb("z_planes", [P, PACK, P], BF16)
         acc = key_products(3, 4)
         for t in range(PACK):
             nc.scalar.activation(z_planes[:, t, :], acc[:, t, :], ACT.Copy, scale=gk_sb[:, t : t + 1])
+        interleave(wv_bf[:, 384:, :], wv_raw[1][:, :, P:], nc.scalar.copy)
         wv_q = mx_pair("wv_q")
         zv_planes = sb("zv_planes", [P, PACK, N], BF16)
 
@@ -186,14 +187,13 @@ def tile_picked_listsmooth_sigmoid_p_kernel(
             if u != 1:
                 nc.sync.dma_start(plains[u], windows[u][:, :V])
 
-        weighted_read(z_bf[0][:], key_products(0, 6), gk_sb)
-        for part in range(2):
-            quantize(z2_q, slice(HALF * part, HALF * (part + 1)), z2_bf[part][:])
+        weighted_read(z_bf[0][:], first_keys, gk_sb)
+        quantize(z2_q, slice(384, V), z2_bf[1][:])
         scores(0)
-        weighted_read(z_bf[1][:], key_products(1, 7), gk_sb)
         interleave(z_bf[3][:], z_planes[:])
-        scores(1)
+        weighted_read(z_bf[1][:], key_products(1, 7), gk_sb)
         scores(3)
+        scores(1)
         weighted_read(z_bf[2][:], key_products(2, 5), gk_sb)
         quantize(wv_q, slice(0, N), wv_bf[:])
         scores(2)

@@ -18,7 +18,9 @@ ALU = mybir.AluOpType
 P = 128
 PACK = 4
 HALF = 256
-RANGES = ((0, 256), (256, 384), (384, 512))
+THREE = 384
+SIXTEENTH = 0.0625
+LAST_PLANE_PIECES = ((0, HALF), (HALF, THREE), (THREE, V))
 
 
 def tile_picked_listsmooth_sigmoid_p_kernel(
@@ -125,16 +127,12 @@ def tile_picked_listsmooth_sigmoid_p_kernel(
         w2_bf = round_dealt("w2", w2_raw)
         w2_q = mx_pair("w2_q")
         quantize(w2_q, slice(0, H), w2_bf[:])
-        for part in range(2):
-            nc.vector.tensor_copy(
-                queries[0][:, HALF * part : HALF * (part + 1)],
-                x_wd[:].bitcast(U32).indirect(qs_sb[:, 16 * part : 16 * (part + 1)]),
-            )
+        nc.vector.tensor_copy(queries[0][:], x_wd[:].bitcast(U32).indirect(qs_sb[:]))
         nc.vector.tensor_copy(keys[0][:].rearrange("p (t m) -> p m t", t=PACK), x_wd[:].bitcast(U32).indirect(offs_sb[:]))
         w1_bf = round_dealt("w1", w1_raw)
         w1_q = mx_pair("w1_q")
 
-        z2_bf = [sb("z2_bf0", [P, 384, PACK], BF16), sb("z2_bf1", [P, P, PACK], BF16, "w1_raw1")]
+        z2_bf = [sb("z2_bf0", [P, THREE, PACK], BF16), sb("z2_bf1", [P, P, PACK], BF16, "w1_raw1")]
 
         def read_queries(c):
             acc = bank(c, [P, PACK, P])
@@ -147,11 +145,11 @@ def tile_picked_listsmooth_sigmoid_p_kernel(
         quantize(w1_q, slice(0, H), w1_bf[:])
         read_queries(3)
         z2_q = (sb("z2_wd", [P, V], U32, "w1_bf"), sb("z2_sc", [P, V], U8))
-        quantize(z2_q, slice(0, 384), z2_bf[0][:])
+        quantize(z2_q, slice(0, THREE), z2_bf[0][:])
 
         wv_bf = sb("wv_bf", [P, N, PACK], BF16)
         interleave(wv_bf[:, :HALF, :], wv_raw[0][:], nc.scalar.copy)
-        interleave(wv_bf[:, HALF:384, :], wv_raw[1][:, :, :P], nc.scalar.copy)
+        interleave(wv_bf[:, HALF:THREE, :], wv_raw[1][:, :, :P], nc.scalar.copy)
         z_q = mx_pair("z_q")
         z_bf = [sb(f"z_bf{u}", [P, P, PACK], BF16) for u in range(PACK)]
 
@@ -163,10 +161,10 @@ def tile_picked_listsmooth_sigmoid_p_kernel(
 
         first_keys = key_products(0, 6)
         z_planes = sb("z_planes", [P, PACK, P], BF16)
-        acc = key_products(3, 4)
+        last_keys = key_products(3, 4)
         for t in range(PACK):
-            nc.scalar.activation(z_planes[:, t, :], acc[:, t, :], ACT.Copy, scale=gk_sb[:, t : t + 1])
-        interleave(wv_bf[:, 384:, :], wv_raw[1][:, :, P:], nc.scalar.copy)
+            nc.scalar.activation(z_planes[:, t, :], last_keys[:, t, :], ACT.Copy, scale=gk_sb[:, t : t + 1])
+        interleave(wv_bf[:, THREE:, :], wv_raw[1][:, :, P:], nc.scalar.copy)
         wv_q = mx_pair("wv_q")
         zv_planes = sb("zv_planes", [P, PACK, N], BF16)
 
@@ -188,7 +186,7 @@ def tile_picked_listsmooth_sigmoid_p_kernel(
                 nc.sync.dma_start(plains[u], windows[u][:, :V])
 
         weighted_read(z_bf[0][:], first_keys, gk_sb)
-        quantize(z2_q, slice(384, V), z2_bf[1][:])
+        quantize(z2_q, slice(THREE, V), z2_bf[1][:])
         scores(0)
         interleave(z_bf[3][:], z_planes[:])
         weighted_read(z_bf[1][:], key_products(1, 7), gk_sb)
@@ -207,13 +205,13 @@ def tile_picked_listsmooth_sigmoid_p_kernel(
 
         gated = sb("gated", [P, PACK, V], F32)
 
-        def gate(u, ranges):
-            joined = sb(f"joined{u}", [P, V], F32)
-            for lo, hi in ranges:
+        def gate(u, pieces, tag=None):
+            joined = sb(f"joined{u}", [P, V], F32, tag)
+            for lo, hi in pieces:
                 nc.vector.tensor_tensor(
                     joined[:, lo:hi], windows[u][:].indirect(nb_sb[:, lo // 16 : hi // 16]), plains[u][:, lo:hi], ALU.add
                 )
-                nc.scalar.activation(gated[:, u, lo:hi], joined[:, lo:hi], ACT.Sigmoid, scale=0.0625)
+                nc.scalar.activation(gated[:, u, lo:hi], joined[:, lo:hi], ACT.Sigmoid, scale=SIXTEENTH)
 
         def weight_on_scalar(u, lo, hi):
             nc.scalar.activation(zp_planes[:, u, lo:hi], gated[:, u, lo:hi], ACT.Copy, scale=gt_sb[:, u : u + 1])
@@ -223,20 +221,24 @@ def tile_picked_listsmooth_sigmoid_p_kernel(
             gate(u, ((0, V),))
             weight_on_scalar(u, HALF, V)
         gate(3, ((0, V),))
-        zv_q = (sb("zv_wd", [P, N], U32, "plain3"), sb("zv_sc", [P, N], U8))
         interleave(zv_bf[:, :HALF, :], zv_planes[:, :, :HALF])
-        quantize(zv_q, slice(0, N), zv_bf[:])
-        gate(2, RANGES)
-        spare = bank(7, [P, N])
+        zv_q = [
+            (sb("zv_wd0", [P, HALF], U32, "joined0"), sb("zv_sc0", [P, HALF], U8)),
+            (sb("zv_wd1", [P, HALF], U32), sb("zv_sc1", [P, HALF], U8)),
+        ]
+        quantize(zv_q[1], slice(0, HALF), zv_bf[:, HALF:, :])
+        gate(2, LAST_PLANE_PIECES, "zv_planes")
+        quantize(zv_q[0], slice(0, HALF), zv_bf[:, :HALF, :])
+        spare = bank(7, [P, V])
         for number in range(2):
-            product(spare[:], zv_q, chunk(number), zv_q, slice(0, N))
+            product(spare[:], zv_q[1], chunk(number), z2_q, slice(0, V))
         weight_on_scalar(3, HALF, V)
-        for lo, hi in RANGES[1:]:
+        for lo, hi in LAST_PLANE_PIECES[1:]:
             weight_on_scalar(2, lo, hi)
         out_view = out.rearrange("(m p) v -> p m v", p=P)
         for lo in range(0, V, P):
             hi = lo + P
-            zp_bf = sb(f"zp_bf{lo}", [P, hi - lo, PACK], BF16)
+            zp_bf = sb(f"zp_bf{lo}", [P, P, PACK], BF16)
             if lo < HALF:
                 nc.vector.tensor_tensor(
                     zp_bf[:].rearrange("p (c i) t -> p c t i", i=4),
@@ -248,18 +250,19 @@ def tile_picked_listsmooth_sigmoid_p_kernel(
                 interleave(zp_bf[:], zp_planes[:, :, lo:hi], nc.scalar.copy)
             quantize(zp_q, slice(lo, hi), zp_bf[:])
 
-        def result(number, m0, rows, lo, hi):
-            acc = bank(number, [P, rows, hi - lo])
-            for m in range(rows):
-                product(acc[:, m, :], zv_q, chunk(m0 + m), zp_q, slice(lo, hi))
-            tile = sb(f"result{number}", [P, rows, hi - lo], F32)
-            nc.vector.scalar_tensor_tensor(tile[:], acc[:], 0.0625, res_sb[:, m0 : m0 + rows, lo:hi], ALU.mult, ALU.add)
-            nc.sync.dma_start(out_view[:, m0 : m0 + rows, lo:hi], tile[:])
+        def result(number, first, blocks, c):
+            acc = bank(number, [P, blocks, P])
+            for m in range(blocks):
+                product(acc[:, m, :], zv_q[(first + m) // 2], chunk((first + m) % 2), zp_q, chunk(c))
+            tile = sb(f"result{number}", [P, blocks, P], F32)
+            rows = slice(first, first + blocks)
+            nc.vector.scalar_tensor_tensor(tile[:], acc[:], SIXTEENTH, res_sb[:, rows, chunk(c)], ALU.mult, ALU.add)
+            nc.sync.dma_start(out_view[:, rows, chunk(c)], tile[:])
 
-        result(0, 0, 1, 0, 128)
-        result(5, 1, 3, 0, 128)
-        result(1, 0, 4, 128, 256)
-        result(2, 0, 4, 256, 384)
-        result(3, 0, 2, 384, 512)
-        result(4, 2, 1, 384, 512)
-        result(6, 3, 1, 384, 512)
+        result(0, 0, 1, 0)
+        result(5, 1, 3, 0)
+        result(1, 0, 4, 1)
+        result(2, 0, 4, 2)
+        result(3, 0, 2, 3)
+        result(4, 2, 1, 3)
+        result(6, 3, 1, 3)

@@ -114,7 +114,10 @@ def tile_picked_listsmooth_sigmoid_p_kernel(
 
         def weighted_read(grouped, acc, gain):
             nc.vector.tensor_tensor(
-                grouped, acc[:].rearrange("p t c -> p c t"), gain[:].unsqueeze(1).to_broadcast([P, P, PACK]), ALU.mult
+                grouped.rearrange("p (c i) t -> p c t i", i=2),
+                acc[:].rearrange("p t (c i) -> p c t i", i=2),
+                gain[:].unsqueeze(1).unsqueeze(3).to_broadcast([P, P // 2, PACK, 2]),
+                ALU.mult,
             )
 
         def interleave(grouped, planes, move=nc.vector.tensor_copy):

from contextlib import ExitStack

import concourse.mybir as mybir

K, T, S, V, N, H = 512, 2048, 512, 512, 512, 512
FLOPS = 2 * K * S * N + 2 * K * H * S + 2 * K * H * V + 2 * H * S * V + 2 * S * N * V

F32 = mybir.dt.float32
BF16 = mybir.dt.bfloat16
I32 = mybir.dt.int32
U32 = mybir.dt.uint32
U16 = mybir.dt.uint16
U8 = mybir.dt.uint8
FP8X4 = mybir.dt.float8_e4m3fn_x4
ACT = mybir.ActivationFunctionType
ALU = mybir.AluOpType

P = 128
PACK = 4
HALF = 256
THREE = 384
SIXTEENTH = 0.0625
LAST_PLANE_PIECES = ((0, HALF), (HALF, THREE), (THREE, V))


def tile_picked_listsmooth_sigmoid_p_kernel(
    tc, x_words, x_scales, w1, w2, gk, gq, wv, gi, res, gt, offs, qs, nb, out
):
    nc = tc.nc
    with ExitStack() as ctx:
        keep = ctx.enter_context(tc.tile_pool(name="keep", bufs=1))
        psum = ctx.enter_context(tc.psum_pool(name="psum", bufs=1))

        def sb(name, shape, dtype, tag=None):
            return keep.tile(shape, dtype, name=name, tag=tag or name, align_bytes=64)

        def bank(number, shape):
            return psum.tile(shape, F32, name=f"bank{number}", tag=f"bank{number}")

        def chunk(c):
            return slice(c * P, (c + 1) * P)

        def load_list(name, src):
            tile = sb(name, [P, 32], U16)
            nc.sync.dma_start(tile[:], src)
            return tile

        def load_gain(name, src):
            tile = sb(name, [P, PACK], F32)
            nc.sync.dma_start(tile[:], src.rearrange("(p t) o -> p (t o)", t=PACK))
            return tile

        def load_halves(halves, w):
            rows = w.rearrange("(p j) c -> p j c", j=PACK)
            for part in range(2):
                nc.sync.dma_start(halves[part][:], rows[:, :, HALF * part : HALF * (part + 1)])

        sc_rows = sb("sc_rows", [P, T // 4], I32)
        x_sc = sb("x_sc", [P, T], U8)
        x_wd = sb("x_wd", [P, T], I32)
        cold = sb("cold", [P, 1], F32)
        warm = sb("warm", [P, 1], F32)
        qs_sb = load_list("qs_sb", qs)
        offs_sb = load_list("offs_sb", offs)
        for q, queue in enumerate((nc.scalar, nc.scalar, nc.scalar, nc.sync)):
            queue.dma_start(sc_rows[32 * q : 32 * q + 4, :], x_scales[0, 4 * q : 4 * q + 4, :].bitcast(I32))
        nc.gpsimd.memset(cold[:], 0.0)
        nc.scalar.activation(warm[:], cold[:], ACT.Sigmoid)
        nc.vector.memset(x_sc[:].bitcast(I32), 0)
        for q in range(4):
            nc.vector.tensor_copy(x_sc[32 * q : 32 * q + 4, :].bitcast(I32), sc_rows[32 * q : 32 * q + 4, :])
        w2_raw = [sb(f"w2_raw{part}", [P, PACK, HALF], F32) for part in range(2)]
        load_halves(w2_raw, w2)
        nc.sync.dma_start(x_wd[:], x_words[0].rearrange("p c r -> p (c r)").bitcast(I32))
        gq_sb = load_gain("gq_sb", gq)
        gk_sb = load_gain("gk_sb", gk)
        w1_raw = [sb(f"w1_raw{part}", [P, PACK, HALF], F32) for part in range(2)]
        load_halves(w1_raw, w1)
        wv_raw = [sb(f"wv_raw{part}", [P, PACK, HALF], F32) for part in range(2)]
        load_halves(wv_raw, wv)
        nb_sb = load_list("nb_sb", nb)
        gi_sb = load_gain("gi_sb", gi)
        gt_sb = load_gain("gt_sb", gt)
        res_sb = sb("res_sb", [P, PACK, V], F32)
        nc.sync.dma_start(res_sb[:], res.rearrange("(m p) v -> p m v", p=P))

        def mx_pair(name):
            return sb(name + "_wd", [P, 512], U32), sb(name + "_sc", [P, 512], U8)

        def quantize(pair, cols, grouped):
            nc.vector.quantize_mx(
                out=pair[0][:, cols].bitcast(FP8X4), scales=pair[1][:, cols], in_=grouped.rearrange("p c j -> p (c j)")
            )

        def product(acc, left, left_cols, right, right_cols):
            nc.tensor.matmul_mx(
                out=acc,
                lhsT=left[0][:, left_cols].bitcast(FP8X4),
                lhsT_scale=left[1][:, left_cols],
                rhs=right[0][:, right_cols].bitcast(FP8X4),
                rhs_scale=right[1][:, right_cols],
                start=True,
                stop=True,
            )

        def round_dealt(name, halves):
            grouped = sb(name + "_bf", [P, 512, PACK], BF16)
            for part in range(2):
                nc.scalar.copy(
                    grouped[:].rearrange("p (t m) j -> p m j t", t=PACK)[:, 64 * part : 64 * (part + 1)],
                    halves[part][:].rearrange("p j (m t) -> p m j t", t=PACK),
                )
            return grouped

        def weighted_read(grouped, acc, gain):
            nc.vector.tensor_tensor(
                grouped.rearrange("p (c i) t -> p c t i", i=2),
                acc[:].rearrange("p t (c i) -> p c t i", i=2),
                gain[:].unsqueeze(1).unsqueeze(3).to_broadcast([P, P // 2, PACK, 2]),
                ALU.mult,
            )

        def interleave(grouped, planes, move=nc.vector.tensor_copy):
            move(grouped.rearrange("p (c i) t -> p c t i", i=4), planes.rearrange("p t (c i) -> p c t i", i=4))

        keys = mx_pair("key")
        queries = mx_pair("query")
        nc.vector.tensor_copy(queries[1][:], x_sc[:].indirect(qs_sb[:]))
        nc.vector.tensor_copy(keys[1][:].rearrange("p (t m) -> p m t", t=PACK), x_sc[:].indirect(offs_sb[:]))
        w2_bf = round_dealt("w2", w2_raw)
        w2_q = mx_pair("w2_q")
        quantize(w2_q, slice(0, H), w2_bf[:])
        nc.vector.tensor_copy(queries[0][:], x_wd[:].bitcast(U32).indirect(qs_sb[:]))
        nc.vector.tensor_copy(keys[0][:].rearrange("p (t m) -> p m t", t=PACK), x_wd[:].bitcast(U32).indirect(offs_sb[:]))
        w1_bf = round_dealt("w1", w1_raw)
        w1_q = mx_pair("w1_q")

        z2_bf = [sb("z2_bf0", [P, THREE, PACK], BF16), sb("z2_bf1", [P, P, PACK], BF16, "w1_raw1")]

        def read_queries(c):
            acc = bank(c, [P, PACK, P])
            for t in range(PACK):
                product(acc[:, t, :], w2_q, chunk(t), queries, chunk(c))
            weighted_read(z2_bf[c // 3][:, chunk(c % 3), :], acc, gq_sb)

        for c in range(3):
            read_queries(c)
        quantize(w1_q, slice(0, H), w1_bf[:])
        read_queries(3)
        z2_q = (sb("z2_wd", [P, V], U32, "w1_bf"), sb("z2_sc", [P, V], U8))
        quantize(z2_q, slice(0, THREE), z2_bf[0][:])

        wv_bf = sb("wv_bf", [P, N, PACK], BF16)
        interleave(wv_bf[:, :HALF, :], wv_raw[0][:], nc.scalar.copy)
        interleave(wv_bf[:, HALF:THREE, :], wv_raw[1][:, :, :P], nc.scalar.copy)
        z_q = mx_pair("z_q")
        z_bf = [sb(f"z_bf{u}", [P, P, PACK], BF16) for u in range(PACK)]

        def key_products(u, number):
            acc = bank(number, [P, PACK, P])
            for t in range(PACK):
                product(acc[:, t, :], w1_q, chunk(t), keys, chunk(u))
            return acc

        first_keys = key_products(0, 6)
        z_planes = sb("z_planes", [P, PACK, P], BF16)
        last_keys = key_products(3, 4)
        for t in range(PACK):
            nc.scalar.activation(z_planes[:, t, :], last_keys[:, t, :], ACT.Copy, scale=gk_sb[:, t : t + 1])
        interleave(wv_bf[:, THREE:, :], wv_raw[1][:, :, P:], nc.scalar.copy)
        wv_q = mx_pair("wv_q")
        zv_planes = sb("zv_planes", [P, PACK, N], BF16)

        def values(u):
            acc = bank(4 + u, [P, N])
            product(acc[:], keys, chunk(u), wv_q, slice(0, N))
            nc.scalar.activation(zv_planes[:, u, :], acc[:], ACT.Copy, scale=gi_sb[:, u : u + 1])

        windows = [sb(f"window{u}", [P, V if u == 2 else 2 * V], F32) for u in range(PACK)]
        nc.vector.memset(windows[1][:, V:], 0.0)
        plains = [windows[3][:, V:], windows[0][:, V:]] + [sb(f"plain{u}", [P, V], F32)[:] for u in (2, 3)]

        def scores(u):
            quantize(z_q, chunk(u), z_bf[u][:])
            acc = bank(u, [P, V])
            product(acc[:], z_q, chunk(u), z2_q, slice(0, V))
            nc.scalar.copy(windows[u][:, :V], acc[:])
            if u != 1:
                nc.sync.dma_start(plains[u], windows[u][:, :V])

        weighted_read(z_bf[0][:], first_keys, gk_sb)
        quantize(z2_q, slice(THREE, V), z2_bf[1][:])
        scores(0)
        interleave(z_bf[3][:], z_planes[:])
        weighted_read(z_bf[1][:], key_products(1, 7), gk_sb)
        scores(3)
        scores(1)
        weighted_read(z_bf[2][:], key_products(2, 5), gk_sb)
        quantize(wv_q, slice(0, N), wv_bf[:])
        scores(2)
        for u in range(PACK):
            values(u)
        zv_bf = sb("zv_bf", [P, N, PACK], BF16)
        interleave(zv_bf[:, HALF:, :], zv_planes[:, :, HALF:], nc.scalar.copy)

        zp_planes = sb("zp_planes", [P, PACK, V], BF16)
        zp_q = mx_pair("zp_q")

        gated = sb("gated", [P, PACK, V], F32)

        def gate(u, pieces, tag=None):
            joined = sb(f"joined{u}", [P, V], F32, tag)
            for lo, hi in pieces:
                nc.vector.tensor_tensor(
                    joined[:, lo:hi], windows[u][:].indirect(nb_sb[:, lo // 16 : hi // 16]), plains[u][:, lo:hi], ALU.add
                )
                nc.scalar.activation(gated[:, u, lo:hi], joined[:, lo:hi], ACT.Sigmoid, scale=SIXTEENTH)

        def weight_on_scalar(u, lo, hi):
            nc.scalar.activation(zp_planes[:, u, lo:hi], gated[:, u, lo:hi], ACT.Copy, scale=gt_sb[:, u : u + 1])

        nc.vector.tensor_copy(plains[1], windows[1][:, :V])
        for u in (1, 0):
            gate(u, ((0, V),))
            weight_on_scalar(u, HALF, V)
        gate(3, ((0, V),))
        interleave(zv_bf[:, :HALF, :], zv_planes[:, :, :HALF])
        zv_q = [
            (sb("zv_wd0", [P, HALF], U32, "joined0"), sb("zv_sc0", [P, HALF], U8)),
            (sb("zv_wd1", [P, HALF], U32), sb("zv_sc1", [P, HALF], U8)),
        ]
        quantize(zv_q[1], slice(0, HALF), zv_bf[:, HALF:, :])
        gate(2, LAST_PLANE_PIECES, "zv_planes")
        quantize(zv_q[0], slice(0, HALF), zv_bf[:, :HALF, :])
        spare = bank(7, [P, V])
        for number in range(2):
            product(spare[:], zv_q[1], chunk(number), z2_q, slice(0, V))
        weight_on_scalar(3, HALF, V)
        for lo, hi in LAST_PLANE_PIECES[1:]:
            weight_on_scalar(2, lo, hi)
        out_view = out.rearrange("(m p) v -> p m v", p=P)
        for lo in range(0, V, P):
            hi = lo + P
            zp_bf = sb(f"zp_bf{lo}", [P, P, PACK], BF16)
            if lo < HALF:
                nc.vector.tensor_tensor(
                    zp_bf[:].rearrange("p (c i) t -> p c t i", i=4),
                    gated[:, :, lo:hi].rearrange("p t (c i) -> p c t i", i=4),
                    gt_sb[:].unsqueeze(1).unsqueeze(3).to_broadcast([P, P // 4, PACK, 4]),
                    ALU.mult,
                )
            else:
                interleave(zp_bf[:], zp_planes[:, :, lo:hi], nc.scalar.copy)
            quantize(zp_q, slice(lo, hi), zp_bf[:])

        def result(number, first, blocks, c):
            acc = bank(number, [P, blocks, P])
            for m in range(blocks):
                product(acc[:, m, :], zv_q[(first + m) // 2], chunk((first + m) % 2), zp_q, chunk(c))
            tile = sb(f"result{number}", [P, blocks, P], F32)
            rows = slice(first, first + blocks)
            nc.vector.scalar_tensor_tensor(tile[:], acc[:], SIXTEENTH, res_sb[:, rows, chunk(c)], ALU.mult, ALU.add)
            nc.sync.dma_start(out_view[:, rows, chunk(c)], tile[:])

        result(0, 0, 1, 0)
        result(5, 1, 3, 0)
        result(1, 0, 4, 1)
        result(2, 0, 4, 2)
        result(3, 0, 2, 3)
        result(4, 2, 1, 3)
        result(6, 3, 1, 3)
